import numpy as np, ml_dtypes
CORES = [5,29,101,125,133,157,229,253]
N = 8
BF = ml_dtypes.bfloat16
def gentries(a):
    return np.ascontiguousarray(a.reshape(8, 16, -1).transpose(0, 2, 1)).reshape(8, -1)
def gtable(e):
    e = np.asarray(e); return np.ascontiguousarray(e.reshape(8, -1, 16).transpose(0, 2, 1)).reshape(128, -1).astype(np.int32)
def f(rng, *shape):
    return (rng.standard_normal(shape, dtype=np.float32) * np.exp2(rng.integers(-2, 3, shape[:-1] + (1,)))).astype(BF)
def wide(rng, *shape):
    v = f(rng, *shape).astype(np.float32); k = shape[:-2] + (1, shape[-1])
    return (v * np.exp2(rng.integers(-6, 7, k)) * (rng.random(k) > 0.0625)).astype(BF)
V, H, M, RO, QN = 3072, 2048, 512, 3, 5
NO = V - 1
BIG = 2.0 ** 40
def grow(rng, par, lab, keep, nn, nm):
    B, q = nm.shape[0], nm.shape[2]; b = np.arange(B); C = np.full((B, M, 16), NO, np.int64)
    for i in range(M):
        up = C[b, par[:, i]]
        cand = np.concatenate([up, nm[:, i]], axis=1)
        use = np.concatenate([(rng.random((B, 16)) < keep[:, i, None]) & (up != NO), np.arange(q)[None, :] < nn[:, i, None]], axis=1)
        o = np.argsort(np.where(use, rng.random(use.shape), 2.0), axis=1)[:, :16]
        e = np.where(np.take_along_axis(use, o, 1), np.take_along_axis(cand, o, 1), NO)
        C[:, i] = np.take_along_axis(e, np.argsort(rng.random((B, 16)), axis=1), 1)
    D = np.empty_like(C); p = np.empty((B, M), np.int64)
    D[b[:, None], lab] = C; p[b[:, None], lab] = np.take_along_axis(lab, par, 1)
    return D, p
def fresh(rng):
    return np.argsort(rng.random((8 * N, V - 1)), axis=1)[:, :M * QN].reshape(8 * N, M, QN)
def shape(rng):
    B = 8 * N; n = np.arange(M)[None, :]; u = rng.random((B, M)); kind = rng.integers(0, 4, (B, 1))
    par = np.where(kind == 0, (u * n).astype(np.int64), np.where(kind == 1, n - 1 - (u * 8).astype(np.int64), np.where(kind == 2, (u * np.minimum(n, 12)).astype(np.int64), np.where(u > 0.7, n - 2, n - 1))))
    return np.maximum(par, 0), np.argsort(rng.random((B, M)), axis=1)
def trees(rng):
    par, lab = shape(rng); B = 8 * N
    keep = rng.choice(np.array([0.4, 0.7, 0.9, 1.0]), (B, M)); nn = np.where(rng.random((B, M)) < 0.15, 0, rng.integers(0, QN + 1, (B, M))); nn[:, 0] = QN
    return grow(rng, par, lab, keep, nn, fresh(rng))
def floats(rng):
    sc = np.exp2(rng.integers(-2, 3, (N, 128, 1))).astype(np.float32)
    x = (rng.standard_normal((N, 128, V), dtype=np.float32) * sc).astype(BF)
    col = np.repeat(1.5 * np.exp2(rng.integers(-3, 3, (N, 8, H))), 16, axis=1).astype(np.float32)
    return x, (np.abs(rng.standard_normal((N, 128, H), dtype=np.float32)) * sc * col).astype(BF)
def pack(x, l, C, p, th):
    C = C.reshape(N, 8, M * 16); p = p.reshape(N, 8, M)
    return {"xs": x, "lim": l, "cq": np.stack([gtable(a) for a in C]), "pt": np.stack([gtable(a) for a in p]), "th": np.asarray(th).astype(np.int32)}
def setup_inputs(rng):
    C, p = trees(rng); x, l = floats(rng)
    return pack(x, l, C, p, rng.integers(4, 17, (N, 8, 2)))
def setup_inputs_corners(rng):
    B = 8 * N; n = np.arange(M); par, lab = shape(rng); g = np.arange(B) & 7; k = (g + np.arange(B) // 8) & 7
    par[k < 2] = np.maximum(n - 1, 0); par[(k == 2) | (k == 3)] = 0; par[k == 4] = np.maximum(n - 1, 0) // 2
    lab[(k == 0) | (k == 2) | (k == 4)] = n; lab[(k == 1) | (k == 3)] = M - 1 - n
    mode = rng.integers(0, 6, (B, M)); mode[g == 5] = 2; mode[g == 6] = 3
    keep = np.array([0.0, 0.0, 1.0, 1.0, 0.93, 0.5])[mode]; nn = np.array([0, QN, 0, QN, 1, QN])[mode]; nn[:, 0] = QN; nn[g == 7, 0] = 0
    C, p = grow(rng, par, lab, keep, nn, fresh(rng)); x, l = floats(rng)
    th = rng.choice(np.array([0, 1, 8, 15, 16]), (N, 8, 2)); th[:, 0, 0] = 0; th[:, 1, 0] = 16; th[:, 5, 1] = 8
    return pack(x, l, C, p, th)
def setup_inputs_hubs(rng):
    B = 8 * N; n = np.arange(M); h = M // 2; k = ((np.arange(B) & 7) + np.arange(B) // 8) & 7
    hub = np.where(n > 1, 1, 0); star = np.zeros_like(n); teeth = np.where(n > h, n - h + 1, 0)
    low = n.copy(); low[0] = 1; low[1] = 0
    high = (n - 2) % M; swap = high.copy(); swap[0] = M - 1; swap[1] = M - 2
    comb = np.where(n > h, 2 * (n - h) - 1, 2 * (n - 1)); comb[0] = M - 1
    par = np.stack([hub, hub, hub, hub, star, star, hub, teeth])[k]; lab = np.stack([low, swap, low, high, M - 1 - n, n, low, comb])[k]
    mode = rng.integers(0, 6, (B, M))
    keep = np.array([0.0, 0.0, 1.0, 1.0, 0.93, 0.5])[mode]; nn = np.array([0, QN, 0, QN, 1, QN])[mode]
    a = (k == 0) | (k == 1); keep[a, 2:] = 0.0; keep[a, 1] = 1.0; nn[a, 1] = QN; keep[a, M - 1] = 1.0; nn[a, M - 1] = 0
    a = k == 6; keep[a, 2:] = np.where((n[2:] >= 3 * M // 4) & (rng.random((N, M - 2)) < 0.125), 0.5, 0.0); keep[a, 1] = 1.0; nn[a, 1] = QN
    a = (k == 2) | (k == 3); keep[a, 1] = 1.0; nn[a, 1] = 0
    a = (k == 4) | (k == 5); keep[a] = 1.0; nn[a] = 0
    a = k == 7; keep[a, 1:h + 1] = 1.0; nn[a, 1:h + 1] = 0
    nn[:, 0] = QN
    C, p = grow(rng, par, lab, keep, nn, fresh(rng)); x, l = floats(rng)
    th = np.stack([rng.choice(np.array([8, 12, 16]), (N, 8)), rng.choice(np.array([0, 8, 16]), (N, 8))], axis=2)
    return pack(x, l, C, p, th)
def setup_inputs_ends(rng):
    B = 8 * N; side = rng.integers(0, 2, (B, 1)); i = np.arange(V - 1)
    lab = np.concatenate([side * (M - 1), (1 - side) * (M - 1), 1 + np.argsort(rng.random((B, M - 2)), axis=1)], axis=1)
    par = rng.integers(0, 2, (B, M)); par[:, :2] = 0
    seq = np.where(i & 1 == 1, i // 2, V - 2 - i // 2); nm = np.full((B, M, QN), NO, np.int64)
    nm[:, 0] = seq[:QN]; nm[:, 1] = seq[QN:2 * QN]; nm[:, 2:, :2] = seq[2 * QN:2 * QN + 2 * (M - 2)].reshape(M - 2, 2)
    keep = np.full((B, M), 0.35); keep[:, 1] = 0.6; nn = rng.integers(0, 3, (B, M)); nn[:, :2] = QN
    C, p = grow(rng, par, lab, keep, nn, nm)
    for c in (0, M - 1):
        C[:, c] = np.sort(C[:, c], axis=1); C[3::4, c] = C[3::4, c, ::-1].copy()
    th = 16 * (np.argsort(rng.random((N, 8, 2)), axis=1) & 1)
    def signs(n, lows):
        kind = rng.integers(0, 2 + lows, (N, 8, 1, n)); kind[..., -2:] = 0
        s = np.where(kind == 0, 1, np.where(kind == 2, -1, 2 * rng.integers(0, 2, (N, 8, 16, n)) - 1))
        return (s * BIG).reshape(N, 128, n).astype(BF)
    return pack(signs(V, 0), signs(H, 1), C, p, th)
def setup_inputs_spread(rng):
    C, p = trees(rng); x = wide(rng, N, 128, V)
    l = np.abs(wide(rng, N, 128, H).astype(np.float32)) * np.where(rng.random((N, 1, H)) < 0.125, -1.0, 1.0)
    return pack(x, l.astype(BF), C, p, rng.integers(0, 17, (N, 8, 2)))
def setup_inputs_ties(rng):
    C, p = trees(rng)
    px = rng.choice(np.array([0.0, 0.75, 1.0, 256.0, -0.25, -1.5 * 2.0 ** -17]), (N, 8, 16, 6)); pl = rng.choice(np.array([0.0, 0.25, 1.0, 255.0, 256.0, 258.0, -1.0]), (N, 8, 16, 8))
    x = np.take_along_axis(px, rng.integers(0, 6, (N, 8, 1, V)), 3); l = np.take_along_axis(pl, rng.integers(0, 8, (N, 8, 1, H)), 3)
    return pack(x.reshape(N, 128, V).astype(BF), l.reshape(N, 128, H).astype(BF), C, p, rng.integers(5, 14, (N, 8, 2)))
def check_inputs(d):
    bad = []
    for k, hi in (("cq", NO), ("pt", M - 1), ("th", 16)):
        if np.min(d[k]) < 0 or np.max(d[k]) > hi: bad.append("range of " + k)
    for k in ("xs", "lim"):
        if not np.all(np.abs(np.asarray(d[k]).astype(np.float32)) <= BIG): bad.append("size of " + k)
    if "range of cq" in bad or "range of pt" in bad: return bad
    g = np.arange(8)[:, None]; own = np.arange(M)[None, :]
    for a in range(N):
        C = gentries(np.asarray(d["cq"][a])).astype(np.int64).reshape(8, M, 16); p = gentries(np.asarray(d["pt"][a])).astype(np.int64)
        e = np.sort(np.where(C == NO, -1 - np.arange(16), C), axis=2)
        if np.any(e[..., 1:] == e[..., :-1]) and "a name twice in a clique of cq" not in bad: bad.append("a name twice in a clique of cq")
        r = p
        for i in range(10): r = np.take_along_axis(r, r, 1)
        if (np.any(r != r[:, :1]) or np.any(np.take_along_axis(p, r, 1) != r)) and "pt not a tree" not in bad: bad.append("pt not a tree")
        inp = np.any(C[:, :, :, None] == C[g, p][:, :, None, :], axis=3)
        top = (C != NO) & (~inp | (p == own)[..., None])
        if np.max(np.bincount((C + V * np.arange(8)[:, None, None])[top], minlength=1)) > 1 and "cliques of a name not connected" not in bad: bad.append("cliques of a name not connected")
    return bad
def reference(xs, lim, cq, pt, th):
    C = np.stack([gentries(a) for a in cq]).astype(np.int64).reshape(N, 8, M, 16); P = np.stack([gentries(a) for a in pt]).astype(np.int64)
    X = xs.astype(np.float32).reshape(N, 8, 16, V); LM = lim.astype(np.float32).reshape(N, 8, 16, H); T = th.astype(np.int64)
    g = np.arange(8)[:, None]; own = np.arange(M)[None, :]; odd = [0] * N
    for t in range(RO):
        c = np.arange(t & 1, M, 2); m = len(c)
        for a in range(N):
            q = (a + t) % N; D = C[a]; pa = P[a]; full = D != NO
            up = D[g, pa]
            same = (D[:, :, :, None] == up[:, :, None, :]) & full[..., None]
            mark = np.any(same, axis=2) & (pa != own)[..., None]
            kids = np.zeros((8, M, 16), np.int64); np.add.at(kids, (g, pa), mark.astype(np.int64))
            e = D[:, c]; Q = up[:, c]; E = same[:, c]; pc = pa[:, c]; act = (pc & 1) != (t & 1)
            outside = full[:, c] & ~np.any(E, axis=3); has = np.any(outside, axis=2)
            y = np.where(has, np.take_along_axis(e, np.argmax(outside, axis=2)[..., None], 2)[..., 0], Q[..., 0])
            h = (((y[..., None] * Q) >> 5) + y[..., None] + 37 * Q) & (H - 1)
            XQ = np.take_along_axis(X[q], Q.reshape(8, 1, -1), 2).reshape(8, 16, m, 16)
            Xy = np.take_along_axis(X[q], y[:, None, :], 2)[..., None]
            LH = np.take_along_axis(LM[q], h.reshape(8, 1, -1), 2).reshape(8, 16, m, 16)
            s = np.add.reduce((np.abs(XQ - Xy) <= LH).astype(np.int64), axis=1)
            inC = np.any(E, axis=2); held = np.any(E & (kids[:, c] > 0)[..., None], axis=2); room = ~full[:, c]
            key = np.where((Q != NO) & ~inC, s, -1); j = np.argmax(key, axis=2); best = np.max(key, axis=2)
            join = act & has & (best >= 0) & (best >= T[q][:, :1] + odd[a]) & np.any(room, axis=2)
            can = inC & ~held; w = np.argmin(np.where(can, s, 17), axis=2)
            leave = act & has & ~join & np.any(can, axis=2); gone = act & ~has
            new = e.copy()
            i, n = np.nonzero(join); new[i, n, np.argmax(room[i, n], axis=1)] = Q[i, n, j[i, n]]
            i, n = np.nonzero(leave); new[i, n, np.argmax(E[i, n, :, w[i, n]], axis=1)] = NO
            i, n = np.nonzero(gone); new[i, n] = np.where(s[i, n] <= T[q][i, 1][:, None], Q[i, n], NO)
            A = np.broadcast_to(own, (8, M)).copy(); A[:, c] = np.where(gone, pc, c[None, :])
            D[:, c] = new; P[a] = np.take_along_axis(A, pa, 1); odd[a] = int(np.count_nonzero(join)) & 1
    return {"yc": np.stack([gtable(a.reshape(8, -1)) for a in C]).astype(np.float32), "yp": np.stack([gtable(a) for a in P]).astype(np.float32)}

@@ -1,0 +1,547 @@
+import math
+import numpy as np
+from concourse.bass import DstId, RemoteDMATransfer
+from concourse.mybir import AluOpType as ALU, ActivationFunctionType as ACT
+
+N = 8
+LO, TO, XO, DW = 0, 2048, 2080, 5152
+ROT = 864
+XP, LP = 776, 512
+LN32 = math.log(32.0)
+ROUNDS = 1500
+PE, FIXV, FIXS, GATHER, LAT = 0.55, 60, 80, 1.55, 120
+POOL = {"hb": ["bfloat16", 0], "hf": ["float16", 0], "ff": ["float32", 0], "ii": ["int32", 0], "uu": ["uint16", 0]}
+SIZE = {"hb": 2, "hf": 2, "ff": 4, "ii": 4, "uu": 2, "d0": 2, "d1": 2, "d2": 2, "xq": 2, "mk": 2, "ks": 2, "ad": 4, "cqi": 4, "pti": 4,
+        "thi": 4, "yco": 4, "ypo": 4}
+for _b in range(8):
+    SIZE["p%d" % _b] = 4
+OPS = []
+
+
+def alloc(pool, n):
+    a = POOL[pool][1]
+    POOL[pool][1] = a + (n + 15) // 16 * 16
+    return (pool, 0, 128, a, a + n, 1)
+
+
+def sub(a, lo, hi, step=1):
+    return (a[0], a[1], a[2], a[3] + lo, a[3] + hi, step)
+
+
+def rows(a, p0, p1):
+    return (a[0], p0, p1, a[3], a[4], a[5])
+
+
+def bank(b, lo=0, hi=512, step=1):
+    return ("p%d" % b, 0, 128, lo, hi, step)
+
+
+def cube(name, n0, n1, j0, j1, w=16):
+    return (name, 0, 128, n0 * w + j0, (n1 - 1) * w + j1, (n0, n1, j0, j1))
+
+
+def ind(win, off):
+    return ("ind", win, off)
+
+
+def count(a):
+    if a[0] == "ind":
+        return 16 * count(a[2])
+    if isinstance(a[5], tuple):
+        return (a[5][1] - a[5][0]) * (a[5][3] - a[5][2])
+    return (a[4] - a[3] + a[5] - 1) // a[5]
+
+
+def isap(a):
+    return isinstance(a, tuple)
+
+
+def psum(a):
+    return a[0][0] == "p" and a[0][1].isdigit()
+
+
+def put(eng, ins, reads, writes, cost, sem=None, val=0):
+    rr = []
+    for a in reads:
+        if isap(a):
+            rr += [a[1], a[2]] if a[0] == "ind" else [a]
+    OPS.append({"eng": eng, "ins": ins, "r": rr, "w": [a for a in writes if isap(a)], "cost": cost, "sem": sem, "val": val})
+
+
+def vcost(out, a, b=None):
+    n = count(out)
+    if a[0] == "ind":
+        return FIXV + GATHER * n
+    if b is not None:
+        return FIXV + max(64, n * (1 if psum(a) or psum(b) else 2))
+    return FIXV + max(64, n * (0.5 if SIZE[out[0]] == 2 and SIZE[a[0]] == 2 else 1))
+
+
+def ts(out, a, s1, o0, s2=None, o1=None):
+    args = (out, a, s1, s2, o0) + ((o1,) if o1 is not None else ())
+    put("v", [("tensor_scalar", args, {})], [a, s1, s2], [out], vcost(out, a))
+
+
+def tt(out, a, b, o):
+    put("v", [("tensor_tensor", (out, a, b, o), {})], [a, b], [out], vcost(out, a, b))
+
+
+def cp(out, a):
+    put("v", [("tensor_copy", (out, a), {})], [a], [out], vcost(out, a))
+
+
+def ms(out, c):
+    put("v", [("memset", (out, c), {})], [], [out], FIXV + max(64, count(out) * SIZE[out[0]] / 4))
+
+
+def act(out, a, f, bias=None, scale=None, acc=None):
+    kw = {k: v for k, v in (("bias", bias), ("scale", scale), ("accum_out", acc)) if v is not None}
+    put("s", [("activation", (out, a, f), kw)], [a, bias, scale], [out, acc], FIXS + max(64, count(out) * (GATHER if a[0] == "ind" else 1)))
+
+
+def mm(lst):
+    c = 30
+    for m in lst:
+        c += PE * max(min(64, count(m[1])), count(m[2])) * (4 if SIZE[m[1][0]] == 4 else 1)
+    put("t", [("matmul", m, {}) for m in lst], [x for m in lst for x in m[1:3]], [m[0] for m in lst], c)
+
+
+def acc(out, terms, first=True, last=True):
+    return [(out, l, r, first and i == 0, last and i == len(terms) - 1) for i, (l, r) in enumerate(terms)]
+
+
+def iota(out, pat, base, mul):
+    kw = {} if out[0] == "ii" else {"allow_small_or_imprecise_dtypes": True}
+    put("g", [("iota", (out, pat, base, mul), kw)], [], [out], 150 + 2 * count(out))
+
+
+def dma(q, out, a, sem, cost):
+    put(q, [("dma_start", (out, a), {})], [a], [out], cost, sem, 16)
+
+
+def build():
+    hb = lambda n: alloc("hb", n)
+    hf = lambda n: alloc("hf", n)
+    ff = lambda n: alloc("ff", n)
+    dat = [("d%d" % t, 0, 128, 0, DW, 1) for t in range(3)]
+    cqi, pti, thi = ("cqi", 0, 128, 0, 512, 1), ("pti", 0, 128, 0, 32, 1), ("thi", 0, 8, 0, 2, 1)
+    yco, ypo = ("yco", 0, 128, 0, 512, 1), ("ypo", 0, 128, 0, 32, 1)
+    hbm = lambda n, lo, hi, p=128: ("@" + n, 0, p, lo, hi, 1)
+    dma("y", pti, hbm("pt", 0, 32), "l_pt", 2000)
+    dma("y", cqi, hbm("cq", 0, 512), "l_cq", 2600)
+    dma("s", sub(dat[0], XO, DW), hbm("xs", 0, 3072), "l_xs", 5500)
+    dma("y", thi, hbm("th", 0, 2, 8), "l_th", 2500)
+    dma("y", sub(dat[0], LO, LO + 2048 - ROT), hbm("lim", ROT, 2048), "l_la", 7000)
+    dma("y", sub(dat[0], LO + 2048 - ROT, TO), hbm("lim", 0, ROT), "l_lb", 7500)
+    for t, tx, tl in ((1, 22000, 27000), (2, 36000, 42000)):
+        put("x", [], [], [sub(dat[t], TO, DW)], tx, "a_x%d" % t, 32)
+        put("x", [], [], [sub(dat[t], LO, TO)], tl, "a_l%d" % t, 32)
+    MAP = ff(512); IO = hb(256); XG = hb(128); XK = hb(128); pi = alloc("ii", 1); ki = alloc("ii", 1)
+    iota(pi, [[1, 1]], 0, 1)
+    iota(XG, [[16, 8], [0, 16]], 0, 0)
+    iota(IO, [[1, 256]], 0, 0)
+    iota(MAP, [[1, 256], [256, 2]], 0, 0)
+    iota(XK, [[0, 8], [1, 16]], 0, 0)
+    pc, kc, g16, g15, gc, k0, p16, pw, kb = [ff(1) for _ in range(9)]
+    cp(pc, pi); ts(ki, pi, 15, ALU.bitwise_and); cp(kc, ki)
+    tt(g16, pc, kc, ALU.subtract); ts(g15, g16, 15.0, ALU.add); ts(gc, g16, 0.0625, ALU.mult)
+    ts(k0, kc, 0.0, ALU.is_equal); ts(p16, pc, 16.0, ALU.mult)
+    BW, BW0 = hf(143), hf(143)
+    ts(BW, sub(IO, 0, 143), g15, ALU.is_equal); ts(BW0, sub(IO, 0, 143), g15, ALU.is_equal, k0, ALU.mult)
+    RS = [hf(128) for _ in range(16)]
+    for j in range(16):
+        ts(RS[j], XG, float(j), ALU.add, pc, ALU.is_equal)
+    I, BLK, NK, WU, TRI, WT, LT, T1, T2, T5, E8 = [hb(128) for _ in range(11)]
+    IH, NIH, BLKH, BLKQ = hf(128), hf(128), hf(128), hf(128)
+    io = sub(IO, 0, 128)
+    ts(I, io, pc, ALU.is_equal); ts(IH, io, pc, ALU.is_equal); ts(NIH, io, pc, ALU.is_equal, -1.0, ALU.mult)
+    ts(BLK, XG, g16, ALU.is_equal); ts(BLKH, XG, g16, ALU.is_equal); ts(BLKQ, XG, g16, ALU.is_equal, 0.5, ALU.mult)
+
+    def times(m, c):
+        o = hb(128); act(o, m, ACT.Copy, scale=c)
+        return o
+
+    NI, N64, P64, N8K, P2K, N64K, P64K, T4 = [times(I, c) for c in (-1.0, -64.0, 64.0, -8192.0, 2048.0, -65536.0, 65536.0, -21.0)]
+    BLKN = times(BLK, -2048.0)
+    act(kb, kc, ACT.Identity, scale=-64.0, bias=-4032.0)
+    pwb = hb(1)
+    act(pwb, kc, ACT.Exp, scale=math.log(2.0)); act(pw, pwb, ACT.Copy)
+    act(T1, XK, ACT.Exp, scale=-math.log(2.0)); tt(NK, T1, BLK, ALU.mult)
+    ts(WU, NK, pw, ALU.mult, 64.0, ALU.mult)
+    WN, W2, NKJ, NK4 = [times(NK, c) for c in (-64.0, 0.5, -65536.0, -16384.0)]
+    ts(T2, XK, kc, ALU.is_gt); tt(LT, T2, BLK, ALU.mult); tt(TRI, LT, N64, ALU.add)
+    T3 = times(LT, 19.0); tt(T5, T3, BLK, ALU.add); tt(WT, T5, T4, ALU.add)
+    B2, BH, B1, B8 = hb(8), hb(8), hb(8), hb(8); B16 = hf(8); i8 = sub(IO, 0, 8)
+    ts(B2, i8, gc, ALU.is_equal, pw, ALU.mult); ts(BH, i8, gc, ALU.is_equal, 0.5, ALU.mult); ts(B1, i8, gc, ALU.is_equal)
+    ts(B16, i8, gc, ALU.is_equal, 0.0625, ALU.mult); ts(B8, i8, gc, ALU.is_equal, -8.0, ALU.mult)
+    ONES = ff(128); C4 = hb(256); CB, CY, CX = hf(256), hf(256), hf(256)
+    ms(ONES, 0.5); ms(C4, 4.0); ms(CY, 170.0); ms(CB, 98.0); ms(CX, -1310.0)
+    TW = ff(768); ms(sub(TW, 256, 512), 0.0)
+    tb = rows(hb(32), 0, 8)
+    ts(rows(E8, 0, 8), rows(XG, 0, 8), rows(p16, 0, 8), ALU.is_equal)
+    ms(tb, 0.0); cp(sub(tb, 0, 2), thi)
+    mm([(bank(7, 0, 32), rows(E8, 0, 8), tb, True, True)])
+    act(sub(dat[0], TO, XO), bank(7, 0, 32), ACT.Copy)
+    put("g", [("sendx", (), {})], [sub(dat[0], TO, DW)], [], 300, "sent", 0)
+    put("g", [("sendl", (), {})], [sub(dat[0], LO, TO)], [], 300, "sent", 0)
+    CW = ff(1024)
+    Qh = [sub(CW, 0, 256), sub(CW, 768, 1024)]; Ch = [sub(CW, 512, 768), sub(CW, 256, 512)]; ZW = [sub(CW, 0, 512), sub(CW, 512, 1024)]
+    H2 = [hf(512), hf(512)]
+    ts(Ch[1], sub(cqi, 1, 512, 2), 32.0, ALU.add)
+    for h in range(2):
+        ts(sub(H2[h], 0, 256), sub(cqi, h, 512, 2), -1536.0, ALU.add); cp(sub(H2[h], 256, 512), sub(H2[h], 0, 256))
+    PB = [hf(512) for _ in range(4)]; PN = hf(512)
+    pl = [alloc("uu", 32) for _ in range(3)]; ql = [alloc("uu", 16) for _ in range(3)]; p0 = alloc("uu", 32)
+    KEY = [hb(32) for _ in range(3)]; HI = [hb(512) for _ in range(2)]
+    OH = [[hb(128) for g in range(8)] for q in range(4)]
+    cp(p0, pti); cp(PN, ind(MAP, p0))
+
+    def lists(t):
+        h = t & 1; mine = bank(6, 16 * h, 16 * h + 16)
+        if t:
+            mm(acc(bank(6, 0, 32), [(sub(BW, 15 - i, 143 - i), sub(PB[t], i, 512, 16)) for i in range(16)]))
+        else:
+            for u in range(2):
+                mm(acc(bank(6, 16 * u, 16 * u + 16), [(sub(BW, 15 - i, 143 - i), sub(PN, u + 2 * i, 512, 32)) for i in range(16)]))
+        if h == 0:
+            ts(ql[t], mine, 0.0625, ALU.mult, -256.0, ALU.add)
+        else:
+            ts(ql[t], mine, 0.0625, ALU.mult, 255.0, ALU.min)
+        ts(pl[t], bank(6, 0, 32), 0.0625, ALU.mult)
+
+    def keys(t):
+        h = t & 1
+        ts(HI[h], PB[t], 256.0 * h + 128, ALU.is_ge)
+        mm([m for q in range(4) for m in acc(bank(6, 32 + 8 * q, 40 + 8 * q),
+            [(sub(PB[t], 128 * q, 128 * q + 128), B16), (sub(HI[h], 128 * q, 128 * q + 128), B8)])])
+        ts(KEY[t], bank(6, 32, 64), -256.0 * h, ALU.add)
+
+    lists(0)
+    for h in range(2):
+        cp(sub(PB[0], 256 * h, 256 * h + 256), sub(PN, h, 512, 2))
+    keys(0)
+    Za, Zb, fe, gq, sq = [hf(256) for _ in range(5)]
+    EQ, SG, IND, XQ, AD = hb(4096), hb(4096), hb(4096), hb(4096), ff(4096)
+    MK, FI, V12 = hb(512), hb(512), hb(512)
+    fE, FE, a64, gone, Wm, ST, KS, Xy, sel1, sw, drop = [hb(256) for _ in range(11)]
+    r1, r2, lvv, n1, r3 = [ff(256) for _ in range(5)]
+    pr, hi = alloc("ii", 256), alloc("ii", 256)
+    qo, ho, yo = alloc("uu", 256), alloc("uu", 256), alloc("uu", 16)
+    cnt = ff(1); oi, oj = alloc("ii", 1), alloc("ii", 1)
+    for t in range(3):
+        h = t & 1; e1 = sub(H2[h], 0, 256); xs = sub(dat[t], TO, DW); lm = sub(dat[t], LO, TO)
+        pa = sub(PB[t], 256 * h, 256 * h + 256); fQ, inC = sub(FI, 0, 256), sub(FI, 256, 512)
+        th1, th2 = sub(dat[t], TO, TO + 1), sub(dat[t], TO + 1, TO + 2)
+        act(Qh[h], ind(Ch[1 - h], ql[t]), ACT.Copy)
+        ts(Za, ind(ZW[h], sub(pl[t], 16 * h, 16 * h + 16)), -1568.0, ALU.add)
+        cp(qo, Qh[h])
+        ts(Zb, ind(ZW[h], sub(pl[t], 16 - 16 * h, 32 - 16 * h)), -1568.0, ALU.add)
+        for c in range(4):
+            act(sub(XQ, 1024 * c, 1024 * c + 1024), ind(xs, sub(qo, 64 * c, 64 * c + 64)), ACT.Copy)
+        if t:
+            act(fE, Ch[h], ACT.Sign, scale=-1.0, bias=3103.0)
+        else:
+            ts(fE, e1, 1535.0, ALU.not_equal)
+        ts(fQ, Za, 1535.0, ALU.not_equal)
+        ts(a64, pa, 256.0, ALU.is_lt if h else ALU.is_ge, 64.0, ALU.mult)
+        for jj in range(8):
+            b = jj & 1
+            mm([(bank(b, 256 * u, 256 * u + 256), RS[2 * jj + u], Za, True, True) for u in range(2)])
+            tt(sub(EQ, 512 * jj, 512 * jj + 512), H2[h], bank(b), ALU.is_equal)
+            mm([(bank(4, 128 * q + j, 128 * q + 128, 16), sub(EQ, 256 * j + 128 * q, 256 * j + 128 * q + 128), B2, True, True)
+                for j in (2 * jj, 2 * jj + 1) for q in range(2)])
+        for jj in range(8):
+            b = 2 + (jj & 1)
+            mm([(bank(b), NIH, H2[1 - h], True, False), (bank(b, 0, 256), RS[2 * jj], Zb, False, False),
+                (bank(b, 256, 512), RS[2 * jj + 1], Zb, False, True)])
+            act(sub(SG, 512 * jj, 512 * jj + 512), bank(b), ACT.Sign)
+            mm([(bank(5, 128 * q + j, 128 * q + 128, 16), sub(SG, 256 * j + 128 * q, 256 * j + 128 * q + 128), BH, True, True)
+                for j in (2 * jj, 2 * jj + 1) for q in range(2)])
+        MA, MB = sub(MK, 256 * h, 256 * h + 256), sub(MK, 256 - 256 * h, 512 - 256 * h)
+        act(MA, bank(4, 0, 256), ACT.Copy)
+        mm([(bank(4, 256 + 128 * q, 384 + 128 * q), sub(MA, 128 * q, 128 * q + 128), I, True, True) for q in range(2)])
+        tt(Wm, fQ, bank(4, 256, 512), ALU.mult)
+        u = bank(6, 0, 256); MG = 1.5 * 2.0 ** 30
+        mm([(bank(6, 256, 512), IH, Za, True, True)] + acc(u, [(WU, fE), (BLK, C4)], True, False)); mm(acc(u, [(WN, Wm)], False, True))
+        tt(gone, a64, u, ALU.is_equal); tt(gq, gone, bank(6, 256, 512), ALU.mult)
+        ts(r1, u, MG, ALU.add, -MG, ALU.add); tt(u, r1, u, ALU.is_equal); tt(fe, e1, u, ALU.mult)
+        yl = bank(4, 0, 16); y1 = bank(6, 256, 512)
+        mm(acc(yl, [(sub(BW0, 15 - i, 143 - i), sub(gq, i, 256, 16)) for i in range(16)], True, False))
+        mm(acc(yl, [(sub(BW, 15 - i, 143 - i), sub(fe, i, 256, 16)) for i in range(16)], False, True))
+        mm(acc(y1, [(BLKH, CY), (RS[0], gq), (BLKH, fe)]))
+        ts(yo, yl, 1568.0, ALU.add)
+        act(Xy, ind(xs, yo), ACT.Copy)
+        tt(pr, Qh[h], y1, ALU.mult); ts(hi, pr, 5, ALU.arith_shift_right, 2047, ALU.bitwise_and); cp(ho, hi)
+        act(inC, Wm, ACT.Sign)
+        mm(acc(bank(0, 0, 256), [(TRI, fE), (I, a64), (N64, gone)]))
+        act(FE, bank(0, 0, 256), ACT.Relu, scale=64.0, bias=kb)
+        s1, s2 = bank(7, 0, 256), bank(7, 256, 512)
+        mm([(bank(7), P64, FI, True, False), (s1, N64, inC, False, False), (s1, BLK, FE, False, False),
+            (s2, I, a64, False, False), (s2, N64, gone, False, False)])
+        Ta = sub(TW, 512 * h, 512 * h + 256)
+        mm(acc(bank(1, 0, 256), [(IH, pa), (NI, IO)] + [(N64, C4)] * h)); tt(Ta, gone, bank(1, 0, 256), ALU.mult)
+        tt(PB[t + 1], ind(sub(TW, 256 * h, 256 * h + 512), pl[t]), PB[t], ALU.add)
+        if t < 2:
+            lists(t + 1); keys(t + 1)
+        else:
+            mm(acc(bank(6, 0, 32), [(sub(BW, 15 - i, 143 - i), sub(PB[3], 256 * (i & 1) + (i >> 1), 256 * (i & 1) + 256, 8)) for i in range(16)]))
+            ya, yb = ff(32), ff(32)
+            ts(ya, bank(6, 0, 32), 4096.0, ALU.is_ge, -511.0, ALU.mult); ts(yb, bank(6, 0, 32), 0.125, ALU.mult)
+            tt(ypo, ya, yb, ALU.add)
+            dma("y", hbm("yp", 0, 32), ypo, "s_yp", 2000)
+        for q in range(4):
+            for g in range(8):
+                ts(OH[q][g], io, sub(KEY[t], 8 * q + g, 8 * q + g + 1), ALU.is_equal)
+        MR = 1.5 * 2.0 ** 23
+        act(r2, bank(5, 0, 256), ACT.Identity, bias=MR); act(r3, r2, ACT.Identity, bias=-MR); tt(MB, r3, bank(5, 0, 256), ALU.not_equal)
+        for u, m in ((0, N64K), (1, P64K)):
+            mm([(bank(2 + u), I, MK, True, False)]
+               + [(bank(2 + u, 128 * q, 128 * q + 128), sub(HI[h], 128 * q, 128 * q + 128), m, False, q == 3) for q in range(4)])
+            act(cube("mk", 0, 32, 16 * u, 16 * u + 16, 32), bank(2 + u), ACT.Relu, bias=-65536.0 if u else None)
+        for g in range(0, 8, 2):
+            mm([m for gg in (g, g + 1) for m in acc(bank(5, 256 + 32 * gg, 288 + 32 * gg),
+                [(OH[q][gg], cube("mk", 8 * q + gg, 8 * q + gg + 1, 0, 32, 32)) for q in range(4)])])
+        for c in range(2):
+            act(sub(KS, 128 * c, 128 * c + 128), cube("p5", 8, 16, 16 * c, 16 * c + 16, 32), ACT.Copy)
+            mm([(bank(7, 256 + 128 * c, 384 + 128 * c), sub(KS, 128 * c, 128 * c + 128), N64, False, False)])
+        s3, b0 = bank(6, 0, 256), bank(6, 256, 512)
+        if t == 2:
+            ms(CB, 96.0); ms(CX, -1312.0)
+        mm(acc(b0, [(BLKH, CB), (IH, e1)]) + [(s3, N64, gone, True, False)])
+        for c in range(4):
+            n0 = 64 * c
+            for u in range(2):
+                mm([(bank(u), I, sub(XQ, 16 * n0 + u, 16 * n0 + 1024, 2), True, False)]
+                   + [(bank(u, j, 512, 8), NI, sub(Xy, n0, n0 + 64), False, j == 7) for j in range(8)])
+                act(sub(AD, 16 * n0 + u, 16 * n0 + 1024, 2), bank(u), ACT.Abs)
+            tt(sub(IND, 16 * n0, 16 * n0 + 1024), ind(lm, sub(ho, n0, n0 + 64)), sub(AD, 16 * n0, 16 * n0 + 1024), ALU.is_ge)
+            if c & 1:
+                q = c >> 1; st = sub(ST, 128 * q, 128 * q + 128)
+                mm([(bank(4, 128 * q + j, 128 * q + 128, 16), sub(IND, 2048 * q + j, 2048 * q + 2048, 16), B1, True, True) for j in range(16)])
+                act(st, bank(4, 128 * q, 128 * q + 128), ACT.Copy)
+                mm([(bank(7, 128 * q, 128 * q + 128), st, I, False, False), (bank(7, 256 + 128 * q, 384 + 128 * q), st, NI, False, q == 1)])
+                mm([(bank(6, 128 * q, 128 * q + 128), st, NI, False, q == 1)])
+        ex, c0, c31, nt2, cc = [ff(1) for _ in range(5)]
+        act(ex, th1, ACT.Exp, scale=LN32, bias=math.log(22.0 / 32)); act(c0, ex, ACT.Copy, scale=-1.0)
+        act(nt2, th2, ACT.Identity, scale=-1.0, bias=-64.5)
+        if t:
+            act(c31, ex, ACT.Copy, scale=-31.0); ts(cc, oj, c31, ALU.mult, c0, ALU.add)
+        else:
+            cc = c0
+        act(sub(V12, 256, 512), s2, ACT.Exp, scale=LN32, bias=-128.0 * LN32)
+        act(sub(V12, 0, 256), s1, ACT.Exp, scale=LN32, bias=-128.0 * LN32)
+        act(drop, s3, ACT.Sign, scale=-1.0, bias=nt2)
+        u1, u2 = bank(0, 0, 256), bank(3, 0, 256)
+        mm([(u2, WT, sub(V12, 256, 512), True, True)])
+        mm([(bank(0, 256, 512), IH, Za, True, True)]); mm([(u1, WT, sub(V12, 0, 256), True, True)])
+        act(sel1, u1, ACT.Sign, scale=-1.0, bias=cc, acc=cnt if t < 2 else None); act(u2, u2, ACT.Sign, scale=-1.0, bias=-2.0 ** -90)
+        tt(sw, Wm, u2, ALU.mult); tt(sq, sel1, bank(0, 256, 512), ALU.mult)
+        A2, X = bank(1, 0, 256), bank(2, 0, 256)
+        mm(acc(A2, [(I, gone), (NK4, C4), (W2, Wm)], True, False)); mm(acc(A2, [(NKJ, sel1), (W2, sw)], False, True))
+        mm(acc(X, [(BLKH, CX), (N64, FE), (BLKQ, Za), (IH, gq), (N8K, gone)], True, False))
+        mm(acc(X, [(P2K, drop), (BLKN, sel1)], False, False)); mm(acc(X, [(BLKQ, sq)], False, True))
+        ts(lvv, A2, 1.0, ALU.is_equal, 3071.0 if t == 2 else 3103.0, ALU.mult)
+        tt(n1, lvv, b0, ALU.max)
+        if t == 2:
+            tt(sub(yco, 0, 512, 2), n1, X, ALU.min)
+            dma("y", hbm("yc", 0, 512), yco, "s_yc", 2500)
+        else:
+            tt(Ch[h], n1, X, ALU.min)
+            ts(e1, Ch[h], -1568.0, ALU.add); cp(sub(H2[h], 256, 512), e1)
+            if t == 1:
+                act(sub(yco, 1, 512, 2), Ch[1], ACT.Identity, bias=-32.0)
+            mm([(bank(5, 0, 1), ONES, cnt, True, True)])
+            cp(oi, bank(5, 0, 1)); ts(oj, oi, 1, ALU.bitwise_and)
+
+
+def meet(a, b):
+    if a[0] == b[0] and isinstance(a[5], tuple) and isinstance(b[5], tuple) and (a[5][3] <= b[5][2] or b[5][3] <= a[5][2]):
+        return False
+    if a[5] == b[5] == 2 and (a[3] - b[3]) % 2:
+        return False
+    return a[0] == b[0] and a[1] < b[2] and b[1] < a[2] and a[3] < b[4] and b[3] < a[4]
+
+
+def schedule():
+    n = len(OPS); dep = [set() for _ in range(n)]
+    for i, o in enumerate(OPS):
+        bi = set(a[0] for a in o["r"] + o["w"] if psum(a))
+        o["b"] = bi
+        for j in range(i):
+            p = OPS[j]
+            hit = any(meet(a, b) for a in o["r"] + o["w"] for b in p["w"]) or any(meet(a, b) for a in o["w"] for b in p["r"])
+            if not hit and bi & p["b"] and (o["eng"] != p["eng"] or o["eng"] == "t"):
+                hit = True
+            if not hit and o["eng"] == p["eng"] and o["eng"] in "gy":
+                hit = None
+            if hit or hit is None:
+                dep[i].add((j, bool(hit)))
+    succ = [[] for _ in range(n)]
+    for i in range(n):
+        for j, w in dep[i]:
+            succ[j].append((i, w))
+    eng = [o["eng"] for o in OPS]; cost = [o["cost"] for o in OPS]
+    hold = [0 if o["eng"] == "x" else 60 if o["sem"] else o["cost"] for o in OPS]
+    lag = lambda j, i, w: (cost[j] + (0 if eng[i] == eng[j] == "t" else LAT)) if w else hold[j]
+    pre = [[(j, lag(j, i, w)) for j, w in dep[i]] for i in range(n)]
+    post = [[(k, lag(i, k, w)) for k, w in succ[i]] for i in range(n)]
+
+    def place(line, t, d):
+        k = 0
+        while k < len(line) and line[k][1] <= t:
+            k += 1
+        while k < len(line) and line[k][0] < t + d:
+            t = line[k][1]; k += 1
+        line.insert(k, (t, t + d))
+        return t
+
+    def forward(key):
+        st = [0.0] * n; lines = {}
+        for i in sorted(range(n), key=lambda i: (key[i], i)):
+            t = max([0.0] + [st[j] + d for j, d in pre[i]])
+            st[i] = place(lines.setdefault(eng[i], []), t, hold[i]) if hold[i] else t
+        return st
+
+    def backward(st):
+        en = [0.0] * n; lines = {}
+        for i in sorted(range(n), key=lambda i: (-st[i], -i)):
+            t = max([cost[i]] + [en[k] + d for k, d in post[i]]) - hold[i]
+            en[i] = (place(lines.setdefault(eng[i], []), t, hold[i]) if hold[i] else t) + hold[i]
+        return [-x for x in en]
+
+    prio = [0.0] * n
+    for i in range(n - 1, -1, -1):
+        prio[i] = max([cost[i]] + [prio[k] + d for k, d in post[i]])
+    rng = np.random.default_rng(1); best = cur = None; key = [-x for x in prio]
+    for it in range(ROUNDS):
+        st = forward(backward(forward(key))); span = max(st[i] + cost[i] for i in range(n))
+        if best is None or span < best[0]:
+            best = (span, st)
+        if cur is None or span < cur[0] + 600 * (1 - it / ROUNDS):
+            cur = (span, st)
+        lo = rng.random() * cur[0]; wid = 3000 + 12000 * rng.random(); jig = rng.random(n) * 2500 * rng.random() * (rng.random(n) < 0.4)
+        key = list(cur[1])
+        for i in range(n):
+            key[i] = max([key[i] + (float(jig[i]) if lo < key[i] < lo + wid else 0.0)] + [key[j] + 1e-3 for j, d in pre[i]])
+    start = best[1]; done = [start[i] + cost[i] for i in range(n)]
+    order = sorted(range(n), key=lambda i: (start[i], i))
+    num = {}; know = {}; snap = [None] * n; tok = [None] * n; prog = []
+    for i in order:
+        o = OPS[i]; e = o["eng"]; kn = know.setdefault(e, {}); waits = []
+        need = {}
+        for j, w in dep[i]:
+            if w and not (e == "t" == OPS[j]["eng"]) and tok[j][1] > need.get(tok[j][0], (0, 0))[0]:
+                need[tok[j][0]] = (tok[j][1], j)
+        for sname, (v, j) in sorted(need.items(), key=lambda z: -done[z[1][1]]):
+            if kn.get(sname, 0) < v:
+                waits.append((sname, v))
+                for s2, v2 in snap[j].items():
+                    kn[s2] = max(kn.get(s2, 0), v2)
+        if o["sem"]:
+            tok[i] = (o["sem"], o["val"])
+        else:
+            num[e] = num.get(e, 0) + 1
+            tok[i] = ("n_" + e, num[e])
+        snap[i] = dict(kn); snap[i][tok[i][0]] = tok[i][1]
+        if e != "x":
+            prog.append((e, waits, o["ins"], tok[i]))
+    return prog, num, max(done), [(start[i], OPS[i]) for i in order]
+
+
+build()
+PROG, NUM, SPAN, TIMES = schedule()
+SCRATCH = {k: ("sbuf", [128, v[1]], v[0]) for k, v in POOL.items()}
+for _t in range(3):
+    SCRATCH["d%d" % _t] = ("sbuf", [128, DW], "bfloat16")
+SCRATCH.update({"mk": ("sbuf", [128, 32, 32], "bfloat16"),
+                "cqi": ("sbuf", [128, 512], "int32"), "pti": ("sbuf", [128, 32], "int32"), "thi": ("sbuf", [128, 2], "int32"),
+                "yco": ("sbuf", [128, 512], "float32"), "ypo": ("sbuf", [128, 32], "float32")})
+for _b in range(8):
+    SCRATCH["p%d" % _b] = ("psum", [128, 16, 32] if _b == 5 else [128, 512], "float32")
+SEMAPHORES = ["n_v", "n_s", "n_t", "n_g", "l_pt", "l_cq", "l_xs", "l_th", "l_la", "l_lb", "a_x1", "a_l1", "a_x2", "a_l2", "s_yp", "s_yc",
+              "sent", "h_x", "h_l"]
+
+
+def real(T, a):
+    if not isap(a):
+        return a
+    if a[0] == "ind":
+        return real(T, a[1]).indirect(real(T, a[2]))
+    t = T[a[0].lstrip("@")]
+    if isinstance(a[5], tuple):
+        return t[:, a[5][0]:a[5][1], a[5][2]:a[5][3]]
+    if a[0] == "p5":
+        if a[4] - a[3] == 1:
+            return t[:, a[3] // 32, a[3] % 32:a[4] % 32]
+        return t[:, a[3] // 32:a[4] // 32, a[3] % 32:32:a[5]] if a[5] != 1 else t[:, a[3] // 32:a[4] // 32, :]
+    return t[a[1]:a[2], a[3]:a[4]:a[5]] if a[5] != 1 else t[a[1]:a[2], a[3]:a[4]]
+
+
+def helpers(T, topo, z):
+    src = T.cores[z]
+    return [c for c in topo.cores_of(src) if T.rank_of(c) is None
+            and all(topo.may_write(c, T.cores[(z - t) % N]) for t in (1, 2))][:4]
+
+
+def call(q, name, args, kw):
+    if name == "matmul":
+        return q.matmul(*args)
+    if name == "tensor_scalar":
+        return q.tensor_scalar(*args)
+    if name == "tensor_tensor":
+        return q.tensor_tensor(*args)
+    if name == "tensor_copy":
+        return q.tensor_copy(*args)
+    if name == "memset":
+        return q.memset(*args)
+    if name == "activation":
+        return q.activation(*args, **kw)
+    if name == "iota":
+        return q.iota(*args, **kw)
+    return q.dma_start(*args)
+
+
+def rank_program(g, core, T, topo):
+    rank = T.rank_of(core)
+    parts = ((TO, XP, "x"), (LO, LP, "l"))
+    if rank is None:
+        for z in range(N):
+            hs = helpers(T, topo, z)
+            if core not in hs:
+                continue
+            i = hs.index(core); share = len(topo.engines(T.cores[z], core)) // len(hs); sent = 0
+            for t in (1, 2):
+                dst = T.cores[(z - t) % N]; rid, pid = topo.addr(dst, core)
+                for o, w, nm in parts:
+                    if t == 1:
+                        g.wait_ge(T.sem["h_" + nm], share)
+                    piece = slice(o + i * w, o + (i + 1) * w)
+                    g.remote_dma(T["d%d" % t][:, piece], T.d0[:, piece], T.sem["a_%s%d" % (nm, t)], T.sem.sent, pid, rid, topo.mask(core, dst))
+                    sent += len(topo.engines(core, dst))
+            g.wait_ge(T.sem.sent, sent)
+        return
+    q = {"v": g.vector, "s": g.scalar, "t": g.tensor, "g": g, "y": g.sync}
+    hs = helpers(T, topo, rank); sent = 0
+    for e, waits, ins, tok in PROG:
+        for s, v in waits:
+            q[e].wait_ge(T.sem[s], v)
+        last = None
+        for name, args, kw in ins:
+            if name.startswith("send"):
+                o, w, nm = parts[0 if name == "sendx" else 1]; tr = []
+                for i, c in enumerate(hs):
+                    en = topo.engines(core, c); k = len(en) // len(hs); rid, pid = topo.addr(c, core)
+                    piece = slice(o + i * w, o + (i + 1) * w)
+                    tr.append(RemoteDMATransfer(dst_ids=[DstId(rid=rid, pnc=pid)], dma_engine_mask=sum(1 << x for x in en[i * k:(i + 1) * k]),
+                                                remote_sem=T.sem["h_" + nm], src=T.d0[:, piece], dst=T.d0[:, piece]))
+                    sent += k
+                g.remote_dma_fused(tr, local_sem=T.sem.sent)
+            else:
+                last = call(q[e], name, [real(T, a) for a in args], {k: real(T, a) for k, a in kw.items()})
+        if last is not None:
+            last.then_inc(T.sem[tok[0]], 16 if name == "dma_start" else 1)
+    g.wait_ge(T.sem.sent, sent)
+    for e in "vstg":
+        g.sync.wait_ge(T.sem["n_" + e], NUM[e])
+    for s in ("s_yp", "s_yc"):
+        g.sync.wait_ge(T.sem[s], 16)

@@ -8,7 +8,8 @@ LO, TO, XO, DW = 0, 2048, 2080, 5152
 ROT = 864
 XP, LP = 776, 512
 LN32 = math.log(32.0)
-ROUNDS = 1500
+ONS = ((), (), ())
+ROUNDS = 2500
 PE, FIXV, FIXS, GATHER, LAT = 0.55, 60, 80, 1.55, 120
 POOL = {"hb": ["bfloat16", 0], "hf": ["float16", 0], "ff": ["float32", 0], "ii": ["int32", 0], "uu": ["uint16", 0]}
 SIZE = {"hb": 2, "hf": 2, "ff": 4, "ii": 4, "uu": 2, "d0": 2, "d1": 2, "d2": 2, "xq": 2, "mk": 2, "ks": 2, "ad": 4, "cqi": 4, "pti": 4,
@@ -48,7 +49,7 @@ def count(a):
     if a[0] == "ind":
         return 16 * count(a[2])
     if isinstance(a[5], tuple):
-        return (a[5][1] - a[5][0]) * (a[5][3] - a[5][2])
+        return (a[5][1] - a[5][0]) * len(range(*a[5][2:]))
     return (a[4] - a[3] + a[5] - 1) // a[5]
 
 
@@ -133,9 +134,6 @@ def build():
     dma("y", thi, hbm("th", 0, 2, 8), "l_th", 2500)
     dma("y", sub(dat[0], LO, LO + 2048 - ROT), hbm("lim", ROT, 2048), "l_la", 7000)
     dma("y", sub(dat[0], LO + 2048 - ROT, TO), hbm("lim", 0, ROT), "l_lb", 7500)
-    for t, tx, tl in ((1, 22000, 27000), (2, 36000, 42000)):
-        put("x", [], [], [sub(dat[t], TO, DW)], tx, "a_x%d" % t, 32)
-        put("x", [], [], [sub(dat[t], LO, TO)], tl, "a_l%d" % t, 32)
     MAP = ff(512); IO = hb(256); XG = hb(128); XK = hb(128); pi = alloc("ii", 1); ki = alloc("ii", 1)
     iota(pi, [[1, 1]], 0, 1)
     iota(XG, [[16, 8], [0, 16]], 0, 0)
@@ -171,19 +169,28 @@ def build():
     WN, W2, NKJ, NK4 = [times(NK, c) for c in (-64.0, 0.5, -65536.0, -16384.0)]
     ts(T2, XK, kc, ALU.is_gt); tt(LT, T2, BLK, ALU.mult); tt(TRI, LT, N64, ALU.add)
     T3 = times(LT, 19.0); tt(T5, T3, BLK, ALU.add); tt(WT, T5, T4, ALU.add)
-    B2, BH, B1, B8 = hb(8), hb(8), hb(8), hb(8); B16 = hf(8); i8 = sub(IO, 0, 8)
-    ts(B2, i8, gc, ALU.is_equal, pw, ALU.mult); ts(BH, i8, gc, ALU.is_equal, 0.5, ALU.mult); ts(B1, i8, gc, ALU.is_equal)
+    P3, P4, N4, T6 = [times(I, c) for c in (3.0, 4.0, -4.0, 2.0)]
+    B256, WM, T7 = times(BLK, 1.0 / 256), times(BLK, pw), times(BLK, 0.5); MJ = hb(128); tt(MJ, T6, T7, ALU.add)
+    B2, BH, B1, B8 = hb(16), hb(8), hb(8), hb(8); B16 = hf(8); i8 = sub(IO, 0, 8); iw = ff(1); iwb = hb(1)
+    act(iwb, kc, ACT.Exp, scale=-math.log(2.0), bias=-math.log(2.0)); act(iw, iwb, ACT.Copy); ts(sub(B2, 8, 16), i8, gc, ALU.is_equal, iw, ALU.mult)
+    ts(sub(B2, 0, 8), i8, gc, ALU.is_equal, pw, ALU.mult); ts(BH, i8, gc, ALU.is_equal, 0.5, ALU.mult); ts(B1, i8, gc, ALU.is_equal)
     ts(B16, i8, gc, ALU.is_equal, 0.0625, ALU.mult); ts(B8, i8, gc, ALU.is_equal, -8.0, ALU.mult)
-    ONES = ff(128); C4 = hb(256); CB, CY, CX = hf(256), hf(256), hf(256)
-    ms(ONES, 0.5); ms(C4, 4.0); ms(CY, 170.0); ms(CB, 98.0); ms(CX, -1310.0)
-    TW = ff(768); ms(sub(TW, 256, 512), 0.0)
+    ONES = ff(128); C4 = hb(256); CB, CY, CX = hb(256), hb(256), hb(256); TW = ff(768)
+    for o, c in ((C4, 4), (CY, 170), (sub(TW, 256, 512), 0)):
+        iota(o, [[0, count(o)]], c, 0)
     tb = rows(hb(32), 0, 8)
     ts(rows(E8, 0, 8), rows(XG, 0, 8), rows(p16, 0, 8), ALU.is_equal)
     ms(tb, 0.0); cp(sub(tb, 0, 2), thi)
     mm([(bank(7, 0, 32), rows(E8, 0, 8), tb, True, True)])
     act(sub(dat[0], TO, XO), bank(7, 0, 32), ACT.Copy)
-    put("g", [("sendx", (), {})], [sub(dat[0], TO, DW)], [], 300, "sent", 0)
-    put("g", [("sendl", (), {})], [sub(dat[0], LO, TO)], [], 300, "sent", 0)
+    gx, gl = ("go", 0, 1, 0, 1, 1), ("go", 0, 1, 1, 2, 1)
+    put("g", [("sendx", (), {})], [sub(dat[0], TO, DW)], [gx], 300, "sent", 0)
+    put("g", [("sendl", (), {})], [sub(dat[0], LO, TO)], [gl], 300, "sent", 0)
+    for o, c in ((CB, 96), (CX, -1312), (ONES, 1)):
+        iota(o, [[0, count(o)]], c, 0)
+    for t, tx, tl in ((1, 21000, 25000), (2, 36000, 40000)):
+        put("x", [], [gx], [sub(dat[t], TO, DW)], tx, "a_x%d" % t, 32)
+        put("x", [], [gl], [sub(dat[t], LO, TO)], tl, "a_l%d" % t, 32)
     CW = ff(1024)
     Qh = [sub(CW, 0, 256), sub(CW, 768, 1024)]; Ch = [sub(CW, 512, 768), sub(CW, 256, 512)]; ZW = [sub(CW, 0, 512), sub(CW, 512, 1024)]
     H2 = [hf(512), hf(512)]
@@ -223,11 +230,11 @@ def build():
     Za, Zb, fe, gq, sq = [hf(256) for _ in range(5)]
     EQ, SG, IND, XQ, AD = hb(4096), hb(4096), hb(4096), hb(4096), ff(4096)
     MK, FI, V12 = hb(512), hb(512), hb(512)
-    fE, FE, a64, gone, Wm, ST, KS, Xy, sel1, sw, drop = [hb(256) for _ in range(11)]
+    fE, FE, a64, gone, Wm, ST, KS, KA, KB, Xy, sel1, sw, drop = [hb(256) for _ in range(13)]
     r1, r2, lvv, n1, r3 = [ff(256) for _ in range(5)]
     pr, hi = alloc("ii", 256), alloc("ii", 256)
     qo, ho, yo = alloc("uu", 256), alloc("uu", 256), alloc("uu", 16)
-    cnt = ff(1); oi, oj = alloc("ii", 1), alloc("ii", 1)
+    nv = [0]; cnt = ff(1); oi, oj = alloc("ii", 1), alloc("ii", 1)
     for t in range(3):
         h = t & 1; e1 = sub(H2[h], 0, 256); xs = sub(dat[t], TO, DW); lm = sub(dat[t], LO, TO)
         pa = sub(PB[t], 256 * h, 256 * h + 256); fQ, inC = sub(FI, 0, 256), sub(FI, 256, 512)
@@ -235,7 +242,8 @@ def build():
         act(Qh[h], ind(Ch[1 - h], ql[t]), ACT.Copy)
         ts(Za, ind(ZW[h], sub(pl[t], 16 * h, 16 * h + 16)), -1568.0, ALU.add)
         cp(qo, Qh[h])
-        ts(Zb, ind(ZW[h], sub(pl[t], 16 - 16 * h, 32 - 16 * h)), -1568.0, ALU.add)
+        if t == 0:
+            ts(Zb, ind(ZW[h], sub(pl[t], 16 - 16 * h, 32 - 16 * h)), -1568.0, ALU.add)
         for c in range(4):
             act(sub(XQ, 1024 * c, 1024 * c + 1024), ind(xs, sub(qo, 64 * c, 64 * c + 64)), ACT.Copy)
         if t:
@@ -246,11 +254,19 @@ def build():
         ts(a64, pa, 256.0, ALU.is_lt if h else ALU.is_ge, 64.0, ALU.mult)
         for jj in range(8):
             b = jj & 1
-            mm([(bank(b, 256 * u, 256 * u + 256), RS[2 * jj + u], Za, True, True) for u in range(2)])
-            tt(sub(EQ, 512 * jj, 512 * jj + 512), H2[h], bank(b), ALU.is_equal)
-            mm([(bank(4, 128 * q + j, 128 * q + 128, 16), sub(EQ, 256 * j + 128 * q, 256 * j + 128 * q + 128), B2, True, True)
+            if jj in ONS[t]:
+                mm([(bank(2), NIH, H2[h], True, False), (bank(2, 0, 256), RS[2 * jj], Za, False, False),
+                    (bank(2, 256, 512), RS[2 * jj + 1], Za, False, True)])
+                act(sub(SG, 512 * jj, 512 * jj + 512), bank(2), ACT.Abs)
+                act(sub(EQ, 512 * jj, 512 * jj + 512), sub(SG, 512 * jj, 512 * jj + 512), ACT.Relu, scale=-1.0, bias=1.0)
+            else:
+                b = nv[0] & 1; nv[0] += 1
+                mm([(bank(b, 256 * u, 256 * u + 256), RS[2 * jj + u], Za, True, True) for u in range(2)])
+                tt(sub(EQ, 512 * jj, 512 * jj + 512), H2[h], bank(b), ALU.is_equal)
+            mm([(("p4", 0, 128, 128 * q + j, 512, (0, 2, 128 * q + j, 128 * q + 128, 16)) if t else bank(4, 128 * q + j, 128 * q + 128, 16),
+                 sub(EQ, 256 * j + 128 * q, 256 * j + 128 * q + 128), B2 if t else sub(B2, 0, 8), True, True)
                 for j in (2 * jj, 2 * jj + 1) for q in range(2)])
-        for jj in range(8):
+        for jj in range(0 if t else 8):
             b = 2 + (jj & 1)
             mm([(bank(b), NIH, H2[1 - h], True, False), (bank(b, 0, 256), RS[2 * jj], Zb, False, False),
                 (bank(b, 256, 512), RS[2 * jj + 1], Zb, False, True)])
@@ -259,6 +275,8 @@ def build():
                 for j in (2 * jj, 2 * jj + 1) for q in range(2)])
         MA, MB = sub(MK, 256 * h, 256 * h + 256), sub(MK, 256 - 256 * h, 512 - 256 * h)
         act(MA, bank(4, 0, 256), ACT.Copy)
+        if t:
+            act(MB, bank(4, 256, 512), ACT.Copy)
         mm([(bank(4, 256 + 128 * q, 384 + 128 * q), sub(MA, 128 * q, 128 * q + 128), I, True, True) for q in range(2)])
         tt(Wm, fQ, bank(4, 256, 512), ALU.mult)
         u = bank(6, 0, 256); MG = 1.5 * 2.0 ** 30
@@ -268,7 +286,7 @@ def build():
         yl = bank(4, 0, 16); y1 = bank(6, 256, 512)
         mm(acc(yl, [(sub(BW0, 15 - i, 143 - i), sub(gq, i, 256, 16)) for i in range(16)], True, False))
         mm(acc(yl, [(sub(BW, 15 - i, 143 - i), sub(fe, i, 256, 16)) for i in range(16)], False, True))
-        mm(acc(y1, [(BLKH, CY), (RS[0], gq), (BLKH, fe)]))
+        mm(acc(y1, [(BLK, CY), (RS[0], gq), (BLKH, fe)]))
         ts(yo, yl, 1568.0, ALU.add)
         act(Xy, ind(xs, yo), ACT.Copy)
         tt(pr, Qh[h], y1, ALU.mult); ts(hi, pr, 5, ALU.arith_shift_right, 2047, ALU.bitwise_and); cp(ho, hi)
@@ -293,21 +311,40 @@ def build():
             for g in range(8):
                 ts(OH[q][g], io, sub(KEY[t], 8 * q + g, 8 * q + g + 1), ALU.is_equal)
         MR = 1.5 * 2.0 ** 23
-        act(r2, bank(5, 0, 256), ACT.Identity, bias=MR); act(r3, r2, ACT.Identity, bias=-MR); tt(MB, r3, bank(5, 0, 256), ALU.not_equal)
-        for u, m in ((0, N64K), (1, P64K)):
-            mm([(bank(2 + u), I, MK, True, False)]
-               + [(bank(2 + u, 128 * q, 128 * q + 128), sub(HI[h], 128 * q, 128 * q + 128), m, False, q == 3) for q in range(4)])
-            act(cube("mk", 0, 32, 16 * u, 16 * u + 16, 32), bank(2 + u), ACT.Relu, bias=-65536.0 if u else None)
-        for g in range(0, 8, 2):
-            mm([m for gg in (g, g + 1) for m in acc(bank(5, 256 + 32 * gg, 288 + 32 * gg),
-                [(OH[q][gg], cube("mk", 8 * q + gg, 8 * q + gg + 1, 0, 32, 32)) for q in range(4)])])
+        kids = lambda o, qs: [mm([m for gg in range(g, g + 8 // len(qs)) for m in acc(bank(5, o + 32 * gg, o + 32 + 32 * gg),
+                                  [(OH[q][gg], cube("mk", 8 * q + gg, 8 * q + gg + 1, 0, 32, 32)) for q in qs])])
+                              for g in range(0, 8, 8 // len(qs))]
+        if t == 0:
+            act(r2, bank(5, 0, 256), ACT.Identity, bias=MR); act(r3, r2, ACT.Identity, bias=-MR); tt(MB, r3, bank(5, 0, 256), ALU.not_equal)
+            for u, m in ((0, N64K), (1, P64K)):
+                mm([(bank(2 + u), I, MK, True, False)]
+                   + [(bank(2 + u, 128 * q, 128 * q + 128), sub(HI[h], 128 * q, 128 * q + 128), m, False, q == 3) for q in range(4)])
+                act(cube("mk", 0, 32, 16 * u, 16 * u + 16, 32), bank(2 + u), ACT.Relu, bias=-65536.0 if u else None)
+            kids(256, range(4))
+        else:
+            kids(0, (2 - 2 * h, 3 - 2 * h))
+            for c in range(2):
+                act(sub(KB, 128 * c, 128 * c + 128), cube("p5", 0, 8, 16 * c, 16 * c + 16, 32), ACT.Sign)
+            mm([(bank(3, 256 + 128 * c, 384 + 128 * c), sub(KB, 128 * c, 128 * c + 128), I, True, True) for c in range(2)])
+            act(KA, bank(3, 256, 512), ACT.Copy)
+            mm([m for c in range(2) for m in acc(bank(3, 128 * c, 128 * c + 128),
+                                                 [(sub(C4, 0, 128), B256), (sub(KA, 128 * c, 128 * c + 128), WM)])])
+            tt(bank(3, 0, 256), MB, bank(3, 0, 256), ALU.mult)
+            act(r2, bank(3, 0, 256), ACT.Identity, bias=MR); act(r3, r2, ACT.Identity, bias=-MR); tt(KB, r3, bank(3, 0, 256), ALU.is_gt)
+            mm([(bank(7, 256 + 128 * c, 384 + 128 * c), sub(KB, 128 * c, 128 * c + 128), N64, False, False) for c in range(2)])
+            for u, m in ((0, N64K), (1, P64K)):
+                mm([(bank(2, 256 * u, 256 * u + 256), I, MA, True, False)]
+                   + [(bank(2, 256 * u + 128 * q, 256 * u + 128 * q + 128), sub(HI[h], 256 * h + 128 * q, 256 * h + 128 * q + 128), m, False, q == 1)
+                      for q in range(2)])
+            for u in range(2):
+                act(cube("mk", 16 * h, 16 * h + 16, 16 * u, 16 * u + 16, 32), bank(2, 256 * u, 256 * u + 256), ACT.Relu, bias=-65536.0 if u else None)
+            kids(256, (2 * h, 2 * h + 1))
         for c in range(2):
             act(sub(KS, 128 * c, 128 * c + 128), cube("p5", 8, 16, 16 * c, 16 * c + 16, 32), ACT.Copy)
             mm([(bank(7, 256 + 128 * c, 384 + 128 * c), sub(KS, 128 * c, 128 * c + 128), N64, False, False)])
         s3, b0 = bank(6, 0, 256), bank(6, 256, 512)
-        if t == 2:
-            ms(CB, 96.0); ms(CX, -1312.0)
-        mm(acc(b0, [(BLKH, CB), (IH, e1)]) + [(s3, N64, gone, True, False)])
+        add32 = [(T7, C4)] * (t < 2)
+        mm(acc(b0, [(BLK, CB), (IH, e1)] + add32) + [(s3, N64, gone, True, False)])
         for c in range(4):
             n0 = 64 * c
             for u in range(2):
@@ -338,7 +375,7 @@ def build():
         tt(sw, Wm, u2, ALU.mult); tt(sq, sel1, bank(0, 256, 512), ALU.mult)
         A2, X = bank(1, 0, 256), bank(2, 0, 256)
         mm(acc(A2, [(I, gone), (NK4, C4), (W2, Wm)], True, False)); mm(acc(A2, [(NKJ, sel1), (W2, sw)], False, True))
-        mm(acc(X, [(BLKH, CX), (N64, FE), (BLKQ, Za), (IH, gq), (N8K, gone)], True, False))
+        mm(acc(X, [(BLK, CX), (N64, FE), (BLKQ, Za), (IH, gq), (N8K, gone)] + add32, True, False))
         mm(acc(X, [(P2K, drop), (BLKN, sel1)], False, False)); mm(acc(X, [(BLKQ, sq)], False, True))
         ts(lvv, A2, 1.0, ALU.is_equal, 3071.0 if t == 2 else 3103.0, ALU.mult)
         tt(n1, lvv, b0, ALU.max)
@@ -347,11 +384,20 @@ def build():
             dma("y", hbm("yc", 0, 512), yco, "s_yc", 2500)
         else:
             tt(Ch[h], n1, X, ALU.min)
-            ts(e1, Ch[h], -1568.0, ALU.add); cp(sub(H2[h], 256, 512), e1)
-            if t == 1:
+            if t == 0:
+                ts(e1, Ch[h], -1568.0, ALU.add); cp(sub(H2[h], 256, 512), e1)
+            else:
                 act(sub(yco, 1, 512, 2), Ch[1], ACT.Identity, bias=-32.0)
+            act(KA, u2, ACT.Copy)
+            mm(acc(bank(3, 256, 512), [(P3, inC), (P4, gone), (N4, drop), (MJ, sel1), (NI, KA)]))
+            act(KB, bank(3, 256, 512), ACT.Relu, bias=3.5)
+            for u, m in ((0, N64K), (1, P64K)):
+                mm([x for q in range(2) for x in acc(bank(3, 256 * u + 128 * q, 256 * u + 128 * q + 128),
+                    [(sub(HI[1 - h], 256 * h + 128 * q, 256 * h + 128 * q + 128), m), (sub(KB, 128 * q, 128 * q + 128), I)])])
+            for u in range(2):
+                act(cube("mk", 16 * h, 16 * h + 16, 16 * u, 16 * u + 16, 32), bank(3, 256 * u, 256 * u + 256), ACT.Relu, bias=-65536.0 if u else None)
             mm([(bank(5, 0, 1), ONES, cnt, True, True)])
-            cp(oi, bank(5, 0, 1)); ts(oj, oi, 1, ALU.bitwise_and)
+            cp(oi, bank(5, 0, 1)); ts(oj, oi, 1, ALU.arith_shift_right, 1, ALU.bitwise_and)
 
 
 def meet(a, b):
@@ -442,7 +488,7 @@ def schedule():
         else:
             num[e] = num.get(e, 0) + 1
             tok[i] = ("n_" + e, num[e])
-        snap[i] = dict(kn); snap[i][tok[i][0]] = tok[i][1]
+        snap[i] = dict(kn) if e != "x" else {}; snap[i][tok[i][0]] = tok[i][1]
         if e != "x":
             prog.append((e, waits, o["ins"], tok[i]))
     return prog, num, max(done), [(start[i], OPS[i]) for i in order]
@@ -457,7 +503,7 @@ SCRATCH.update({"mk": ("sbuf", [128, 32, 32], "bfloat16"),
                 "cqi": ("sbuf", [128, 512], "int32"), "pti": ("sbuf", [128, 32], "int32"), "thi": ("sbuf", [128, 2], "int32"),
                 "yco": ("sbuf", [128, 512], "float32"), "ypo": ("sbuf", [128, 32], "float32")})
 for _b in range(8):
-    SCRATCH["p%d" % _b] = ("psum", [128, 16, 32] if _b == 5 else [128, 512], "float32")
+    SCRATCH["p%d" % _b] = ("psum", {4: [128, 2, 256], 5: [128, 16, 32]}.get(_b, [128, 512]), "float32")
 SEMAPHORES = ["n_v", "n_s", "n_t", "n_g", "l_pt", "l_cq", "l_xs", "l_th", "l_la", "l_lb", "a_x1", "a_l1", "a_x2", "a_l2", "s_yp", "s_yc",
               "sent", "h_x", "h_l"]
 
@@ -469,7 +515,9 @@ def real(T, a):
         return real(T, a[1]).indirect(real(T, a[2]))
     t = T[a[0].lstrip("@")]
     if isinstance(a[5], tuple):
-        return t[:, a[5][0]:a[5][1], a[5][2]:a[5][3]]
+        return t[:, a[5][0]:a[5][1], slice(*a[5][2:])]
+    if a[0] == "p4":
+        return t[:, a[3] // 256, slice(a[3] % 256, (a[4] - 1) % 256 + 1, a[5] if a[5] != 1 else None)]
     if a[0] == "p5":
         if a[4] - a[3] == 1:
             return t[:, a[3] // 32, a[3] % 32:a[4] % 32]

import math
import numpy as np
from concourse.bass import DstId, RemoteDMATransfer
from concourse.mybir import AluOpType as ALU, ActivationFunctionType as ACT

N = 8
LO, TO, XO, DW = 0, 2048, 2080, 5152
ROT = 864
XP, LP = 776, 512
LN32 = math.log(32.0)
ONS = ((), (), ())
ROUNDS = 2500
PE, FIXV, FIXS, GATHER, LAT = 0.55, 60, 80, 1.55, 120
POOL = {"hb": ["bfloat16", 0], "hf": ["float16", 0], "ff": ["float32", 0], "ii": ["int32", 0], "uu": ["uint16", 0]}
SIZE = {"hb": 2, "hf": 2, "ff": 4, "ii": 4, "uu": 2, "d0": 2, "d1": 2, "d2": 2, "xq": 2, "mk": 2, "ks": 2, "ad": 4, "cqi": 4, "pti": 4,
        "thi": 4, "yco": 4, "ypo": 4}
for _b in range(8):
    SIZE["p%d" % _b] = 4
OPS = []


def alloc(pool, n):
    a = POOL[pool][1]
    POOL[pool][1] = a + (n + 15) // 16 * 16
    return (pool, 0, 128, a, a + n, 1)


def sub(a, lo, hi, step=1):
    return (a[0], a[1], a[2], a[3] + lo, a[3] + hi, step)


def rows(a, p0, p1):
    return (a[0], p0, p1, a[3], a[4], a[5])


def bank(b, lo=0, hi=512, step=1):
    return ("p%d" % b, 0, 128, lo, hi, step)


def cube(name, n0, n1, j0, j1, w=16):
    return (name, 0, 128, n0 * w + j0, (n1 - 1) * w + j1, (n0, n1, j0, j1))


def ind(win, off):
    return ("ind", win, off)


def count(a):
    if a[0] == "ind":
        return 16 * count(a[2])
    if isinstance(a[5], tuple):
        return (a[5][1] - a[5][0]) * len(range(*a[5][2:]))
    return (a[4] - a[3] + a[5] - 1) // a[5]


def isap(a):
    return isinstance(a, tuple)


def psum(a):
    return a[0][0] == "p" and a[0][1].isdigit()


def put(eng, ins, reads, writes, cost, sem=None, val=0):
    rr = []
    for a in reads:
        if isap(a):
            rr += [a[1], a[2]] if a[0] == "ind" else [a]
    OPS.append({"eng": eng, "ins": ins, "r": rr, "w": [a for a in writes if isap(a)], "cost": cost, "sem": sem, "val": val})


def vcost(out, a, b=None):
    n = count(out)
    if a[0] == "ind":
        return FIXV + GATHER * n
    if b is not None:
        return FIXV + max(64, n * (1 if psum(a) or psum(b) else 2))
    return FIXV + max(64, n * (0.5 if SIZE[out[0]] == 2 and SIZE[a[0]] == 2 else 1))


def ts(out, a, s1, o0, s2=None, o1=None):
    args = (out, a, s1, s2, o0) + ((o1,) if o1 is not None else ())
    put("v", [("tensor_scalar", args, {})], [a, s1, s2], [out], vcost(out, a))


def tt(out, a, b, o):
    put("v", [("tensor_tensor", (out, a, b, o), {})], [a, b], [out], vcost(out, a, b))


def cp(out, a):
    put("v", [("tensor_copy", (out, a), {})], [a], [out], vcost(out, a))


def ms(out, c):
    put("v", [("memset", (out, c), {})], [], [out], FIXV + max(64, count(out) * SIZE[out[0]] / 4))


def act(out, a, f, bias=None, scale=None, acc=None):
    kw = {k: v for k, v in (("bias", bias), ("scale", scale), ("accum_out", acc)) if v is not None}
    put("s", [("activation", (out, a, f), kw)], [a, bias, scale], [out, acc], FIXS + max(64, count(out) * (GATHER if a[0] == "ind" else 1)))


def mm(lst):
    c = 30
    for m in lst:
        c += PE * max(min(64, count(m[1])), count(m[2])) * (4 if SIZE[m[1][0]] == 4 else 1)
    put("t", [("matmul", m, {}) for m in lst], [x for m in lst for x in m[1:3]], [m[0] for m in lst], c)


def acc(out, terms, first=True, last=True):
    return [(out, l, r, first and i == 0, last and i == len(terms) - 1) for i, (l, r) in enumerate(terms)]


def iota(out, pat, base, mul):
    kw = {} if out[0] == "ii" else {"allow_small_or_imprecise_dtypes": True}
    put("g", [("iota", (out, pat, base, mul), kw)], [], [out], 150 + 2 * count(out))


def dma(q, out, a, sem, cost):
    put(q, [("dma_start", (out, a), {})], [a], [out], cost, sem, 16)


def build():
    hb = lambda n: alloc("hb", n)
    hf = lambda n: alloc("hf", n)
    ff = lambda n: alloc("ff", n)
    dat = [("d%d" % t, 0, 128, 0, DW, 1) for t in range(3)]
    cqi, pti, thi = ("cqi", 0, 128, 0, 512, 1), ("pti", 0, 128, 0, 32, 1), ("thi", 0, 8, 0, 2, 1)
    yco, ypo = ("yco", 0, 128, 0, 512, 1), ("ypo", 0, 128, 0, 32, 1)
    hbm = lambda n, lo, hi, p=128: ("@" + n, 0, p, lo, hi, 1)
    dma("y", pti, hbm("pt", 0, 32), "l_pt", 2000)
    dma("y", cqi, hbm("cq", 0, 512), "l_cq", 2600)
    dma("s", sub(dat[0], XO, DW), hbm("xs", 0, 3072), "l_xs", 5500)
    dma("y", thi, hbm("th", 0, 2, 8), "l_th", 2500)
    dma("y", sub(dat[0], LO, LO + 2048 - ROT), hbm("lim", ROT, 2048), "l_la", 7000)
    dma("y", sub(dat[0], LO + 2048 - ROT, TO), hbm("lim", 0, ROT), "l_lb", 7500)
    MAP = ff(512); IO = hb(256); XG = hb(128); XK = hb(128); pi = alloc("ii", 1); ki = alloc("ii", 1)
    iota(pi, [[1, 1]], 0, 1)
    iota(XG, [[16, 8], [0, 16]], 0, 0)
    iota(IO, [[1, 256]], 0, 0)
    iota(MAP, [[1, 256], [256, 2]], 0, 0)
    iota(XK, [[0, 8], [1, 16]], 0, 0)
    pc, kc, g16, g15, gc, k0, p16, pw, kb = [ff(1) for _ in range(9)]
    cp(pc, pi); ts(ki, pi, 15, ALU.bitwise_and); cp(kc, ki)
    tt(g16, pc, kc, ALU.subtract); ts(g15, g16, 15.0, ALU.add); ts(gc, g16, 0.0625, ALU.mult)
    ts(k0, kc, 0.0, ALU.is_equal); ts(p16, pc, 16.0, ALU.mult)
    BW, BW0 = hf(143), hf(143)
    ts(BW, sub(IO, 0, 143), g15, ALU.is_equal); ts(BW0, sub(IO, 0, 143), g15, ALU.is_equal, k0, ALU.mult)
    RS = [hf(128) for _ in range(16)]
    for j in range(16):
        ts(RS[j], XG, float(j), ALU.add, pc, ALU.is_equal)
    I, BLK, NK, WU, TRI, WT, LT, T1, T2, T5, E8 = [hb(128) for _ in range(11)]
    IH, NIH, BLKH, BLKQ = hf(128), hf(128), hf(128), hf(128)
    io = sub(IO, 0, 128)
    ts(I, io, pc, ALU.is_equal); ts(IH, io, pc, ALU.is_equal); ts(NIH, io, pc, ALU.is_equal, -1.0, ALU.mult)
    ts(BLK, XG, g16, ALU.is_equal); ts(BLKH, XG, g16, ALU.is_equal); ts(BLKQ, XG, g16, ALU.is_equal, 0.5, ALU.mult)

    def times(m, c):
        o = hb(128); act(o, m, ACT.Copy, scale=c)
        return o

    NI, N64, P64, N8K, P2K, N64K, P64K, T4 = [times(I, c) for c in (-1.0, -64.0, 64.0, -8192.0, 2048.0, -65536.0, 65536.0, -21.0)]
    BLKN = times(BLK, -2048.0)
    act(kb, kc, ACT.Identity, scale=-64.0, bias=-4032.0)
    pwb = hb(1)
    act(pwb, kc, ACT.Exp, scale=math.log(2.0)); act(pw, pwb, ACT.Copy)
    act(T1, XK, ACT.Exp, scale=-math.log(2.0)); tt(NK, T1, BLK, ALU.mult)
    ts(WU, NK, pw, ALU.mult, 64.0, ALU.mult)
    WN, W2, NKJ, NK4 = [times(NK, c) for c in (-64.0, 0.5, -65536.0, -16384.0)]
    ts(T2, XK, kc, ALU.is_gt); tt(LT, T2, BLK, ALU.mult); tt(TRI, LT, N64, ALU.add)
    T3 = times(LT, 19.0); tt(T5, T3, BLK, ALU.add); tt(WT, T5, T4, ALU.add)
    P3, P4, N4, T6 = [times(I, c) for c in (3.0, 4.0, -4.0, 2.0)]
    B256, WM, T7 = times(BLK, 1.0 / 256), times(BLK, pw), times(BLK, 0.5); MJ = hb(128); tt(MJ, T6, T7, ALU.add)
    B2, BH, B1, B8 = hb(16), hb(8), hb(8), hb(8); B16 = hf(8); i8 = sub(IO, 0, 8); iw = ff(1); iwb = hb(1)
    act(iwb, kc, ACT.Exp, scale=-math.log(2.0), bias=-math.log(2.0)); act(iw, iwb, ACT.Copy); ts(sub(B2, 8, 16), i8, gc, ALU.is_equal, iw, ALU.mult)
    ts(sub(B2, 0, 8), i8, gc, ALU.is_equal, pw, ALU.mult); ts(BH, i8, gc, ALU.is_equal, 0.5, ALU.mult); ts(B1, i8, gc, ALU.is_equal)
    ts(B16, i8, gc, ALU.is_equal, 0.0625, ALU.mult); ts(B8, i8, gc, ALU.is_equal, -8.0, ALU.mult)
    ONES = ff(128); C4 = hb(256); CB, CY, CX = hb(256), hb(256), hb(256); TW = ff(768)
    for o, c in ((C4, 4), (CY, 170), (sub(TW, 256, 512), 0)):
        iota(o, [[0, count(o)]], c, 0)
    tb = rows(hb(32), 0, 8)
    ts(rows(E8, 0, 8), rows(XG, 0, 8), rows(p16, 0, 8), ALU.is_equal)
    ms(tb, 0.0); cp(sub(tb, 0, 2), thi)
    mm([(bank(7, 0, 32), rows(E8, 0, 8), tb, True, True)])
    act(sub(dat[0], TO, XO), bank(7, 0, 32), ACT.Copy)
    gx, gl = ("go", 0, 1, 0, 1, 1), ("go", 0, 1, 1, 2, 1)
    put("g", [("sendx", (), {})], [sub(dat[0], TO, DW)], [gx], 300, "sent", 0)
    put("g", [("sendl", (), {})], [sub(dat[0], LO, TO)], [gl], 300, "sent", 0)
    for o, c in ((CB, 96), (CX, -1312), (ONES, 1)):
        iota(o, [[0, count(o)]], c, 0)
    for t, tx, tl in ((1, 21000, 25000), (2, 36000, 40000)):
        put("x", [], [gx], [sub(dat[t], TO, DW)], tx, "a_x%d" % t, 32)
        put("x", [], [gl], [sub(dat[t], LO, TO)], tl, "a_l%d" % t, 32)
    CW = ff(1024)
    Qh = [sub(CW, 0, 256), sub(CW, 768, 1024)]; Ch = [sub(CW, 512, 768), sub(CW, 256, 512)]; ZW = [sub(CW, 0, 512), sub(CW, 512, 1024)]
    H2 = [hf(512), hf(512)]
    ts(Ch[1], sub(cqi, 1, 512, 2), 32.0, ALU.add)
    for h in range(2):
        ts(sub(H2[h], 0, 256), sub(cqi, h, 512, 2), -1536.0, ALU.add); cp(sub(H2[h], 256, 512), sub(H2[h], 0, 256))
    PB = [hf(512) for _ in range(4)]; PN = hf(512)
    pl = [alloc("uu", 32) for _ in range(3)]; ql = [alloc("uu", 16) for _ in range(3)]; p0 = alloc("uu", 32)
    KEY = [hb(32) for _ in range(3)]; HI = [hb(512) for _ in range(2)]
    OH = [[hb(128) for g in range(8)] for q in range(4)]
    cp(p0, pti); cp(PN, ind(MAP, p0))

    def lists(t):
        h = t & 1; mine = bank(6, 16 * h, 16 * h + 16)
        if t:
            mm(acc(bank(6, 0, 32), [(sub(BW, 15 - i, 143 - i), sub(PB[t], i, 512, 16)) for i in range(16)]))
        else:
            for u in range(2):
                mm(acc(bank(6, 16 * u, 16 * u + 16), [(sub(BW, 15 - i, 143 - i), sub(PN, u + 2 * i, 512, 32)) for i in range(16)]))
        if h == 0:
            ts(ql[t], mine, 0.0625, ALU.mult, -256.0, ALU.add)
        else:
            ts(ql[t], mine, 0.0625, ALU.mult, 255.0, ALU.min)
        ts(pl[t], bank(6, 0, 32), 0.0625, ALU.mult)

    def keys(t):
        h = t & 1
        ts(HI[h], PB[t], 256.0 * h + 128, ALU.is_ge)
        mm([m for q in range(4) for m in acc(bank(6, 32 + 8 * q, 40 + 8 * q),
            [(sub(PB[t], 128 * q, 128 * q + 128), B16), (sub(HI[h], 128 * q, 128 * q + 128), B8)])])
        ts(KEY[t], bank(6, 32, 64), -256.0 * h, ALU.add)

    lists(0)
    for h in range(2):
        cp(sub(PB[0], 256 * h, 256 * h + 256), sub(PN, h, 512, 2))
    keys(0)
    Za, Zb, fe, gq, sq = [hf(256) for _ in range(5)]
    EQ, SG, IND, XQ, AD = hb(4096), hb(4096), hb(4096), hb(4096), ff(4096)
    MK, FI, V12 = hb(512), hb(512), hb(512)
    fE, FE, a64, gone, Wm, ST, KS, KA, KB, Xy, sel1, sw, drop = [hb(256) for _ in range(13)]
    r1, r2, lvv, n1, r3 = [ff(256) for _ in range(5)]
    pr, hi = alloc("ii", 256), alloc("ii", 256)
    qo, ho, yo = alloc("uu", 256), alloc("uu", 256), alloc("uu", 16)
    nv = [0]; cnt = ff(1); oi, oj = alloc("ii", 1), alloc("ii", 1)
    for t in range(3):
        h = t & 1; e1 = sub(H2[h], 0, 256); xs = sub(dat[t], TO, DW); lm = sub(dat[t], LO, TO)
        pa = sub(PB[t], 256 * h, 256 * h + 256); fQ, inC = sub(FI, 0, 256), sub(FI, 256, 512)
        th1, th2 = sub(dat[t], TO, TO + 1), sub(dat[t], TO + 1, TO + 2)
        act(Qh[h], ind(Ch[1 - h], ql[t]), ACT.Copy)
        ts(Za, ind(ZW[h], sub(pl[t], 16 * h, 16 * h + 16)), -1568.0, ALU.add)
        cp(qo, Qh[h])
        if t == 0:
            ts(Zb, ind(ZW[h], sub(pl[t], 16 - 16 * h, 32 - 16 * h)), -1568.0, ALU.add)
        for c in range(4):
            act(sub(XQ, 1024 * c, 1024 * c + 1024), ind(xs, sub(qo, 64 * c, 64 * c + 64)), ACT.Copy)
        if t:
            act(fE, Ch[h], ACT.Sign, scale=-1.0, bias=3103.0)
        else:
            ts(fE, e1, 1535.0, ALU.not_equal)
        ts(fQ, Za, 1535.0, ALU.not_equal)
        ts(a64, pa, 256.0, ALU.is_lt if h else ALU.is_ge, 64.0, ALU.mult)
        for jj in range(8):
            b = jj & 1
            if jj in ONS[t]:
                mm([(bank(2), NIH, H2[h], True, False), (bank(2, 0, 256), RS[2 * jj], Za, False, False),
                    (bank(2, 256, 512), RS[2 * jj + 1], Za, False, True)])
                act(sub(SG, 512 * jj, 512 * jj + 512), bank(2), ACT.Abs)
                act(sub(EQ, 512 * jj, 512 * jj + 512), sub(SG, 512 * jj, 512 * jj + 512), ACT.Relu, scale=-1.0, bias=1.0)
            else:
                b = nv[0] & 1; nv[0] += 1
                mm([(bank(b, 256 * u, 256 * u + 256), RS[2 * jj + u], Za, True, True) for u in range(2)])
                tt(sub(EQ, 512 * jj, 512 * jj + 512), H2[h], bank(b), ALU.is_equal)
            mm([(("p4", 0, 128, 128 * q + j, 512, (0, 2, 128 * q + j, 128 * q + 128, 16)) if t else bank(4, 128 * q + j, 128 * q + 128, 16),
                 sub(EQ, 256 * j + 128 * q, 256 * j + 128 * q + 128), B2 if t else sub(B2, 0, 8), True, True)
                for j in (2 * jj, 2 * jj + 1) for q in range(2)])
        for jj in range(0 if t else 8):
            b = 2 + (jj & 1)
            mm([(bank(b), NIH, H2[1 - h], True, False), (bank(b, 0, 256), RS[2 * jj], Zb, False, False),
                (bank(b, 256, 512), RS[2 * jj + 1], Zb, False, True)])
            act(sub(SG, 512 * jj, 512 * jj + 512), bank(b), ACT.Sign)
            mm([(bank(5, 128 * q + j, 128 * q + 128, 16), sub(SG, 256 * j + 128 * q, 256 * j + 128 * q + 128), BH, True, True)
                for j in (2 * jj, 2 * jj + 1) for q in range(2)])
        MA, MB = sub(MK, 256 * h, 256 * h + 256), sub(MK, 256 - 256 * h, 512 - 256 * h)
        act(MA, bank(4, 0, 256), ACT.Copy)
        if t:
            act(MB, bank(4, 256, 512), ACT.Copy)
        mm([(bank(4, 256 + 128 * q, 384 + 128 * q), sub(MA, 128 * q, 128 * q + 128), I, True, True) for q in range(2)])
        tt(Wm, fQ, bank(4, 256, 512), ALU.mult)
        u = bank(6, 0, 256); MG = 1.5 * 2.0 ** 30
        mm([(bank(6, 256, 512), IH, Za, True, True)] + acc(u, [(WU, fE), (BLK, C4)], True, False)); mm(acc(u, [(WN, Wm)], False, True))
        tt(gone, a64, u, ALU.is_equal); tt(gq, gone, bank(6, 256, 512), ALU.mult)
        ts(r1, u, MG, ALU.add, -MG, ALU.add); tt(u, r1, u, ALU.is_equal); tt(fe, e1, u, ALU.mult)
        yl = bank(4, 0, 16); y1 = bank(6, 256, 512)
        mm(acc(yl, [(sub(BW0, 15 - i, 143 - i), sub(gq, i, 256, 16)) for i in range(16)], True, False))
        mm(acc(yl, [(sub(BW, 15 - i, 143 - i), sub(fe, i, 256, 16)) for i in range(16)], False, True))
        mm(acc(y1, [(BLK, CY), (RS[0], gq), (BLKH, fe)]))
        ts(yo, yl, 1568.0, ALU.add)
        act(Xy, ind(xs, yo), ACT.Copy)
        tt(pr, Qh[h], y1, ALU.mult); ts(hi, pr, 5, ALU.arith_shift_right, 2047, ALU.bitwise_and); cp(ho, hi)
        act(inC, Wm, ACT.Sign)
        mm(acc(bank(0, 0, 256), [(TRI, fE), (I, a64), (N64, gone)]))
        act(FE, bank(0, 0, 256), ACT.Relu, scale=64.0, bias=kb)
        s1, s2 = bank(7, 0, 256), bank(7, 256, 512)
        mm([(bank(7), P64, FI, True, False), (s1, N64, inC, False, False), (s1, BLK, FE, False, False),
            (s2, I, a64, False, False), (s2, N64, gone, False, False)])
        Ta = sub(TW, 512 * h, 512 * h + 256)
        mm(acc(bank(1, 0, 256), [(IH, pa), (NI, IO)] + [(N64, C4)] * h)); tt(Ta, gone, bank(1, 0, 256), ALU.mult)
        tt(PB[t + 1], ind(sub(TW, 256 * h, 256 * h + 512), pl[t]), PB[t], ALU.add)
        if t < 2:
            lists(t + 1); keys(t + 1)
        else:
            mm(acc(bank(6, 0, 32), [(sub(BW, 15 - i, 143 - i), sub(PB[3], 256 * (i & 1) + (i >> 1), 256 * (i & 1) + 256, 8)) for i in range(16)]))
            ya, yb = ff(32), ff(32)
            ts(ya, bank(6, 0, 32), 4096.0, ALU.is_ge, -511.0, ALU.mult); ts(yb, bank(6, 0, 32), 0.125, ALU.mult)
            tt(ypo, ya, yb, ALU.add)
            dma("y", hbm("yp", 0, 32), ypo, "s_yp", 2000)
        for q in range(4):
            for g in range(8):
                ts(OH[q][g], io, sub(KEY[t], 8 * q + g, 8 * q + g + 1), ALU.is_equal)
        MR = 1.5 * 2.0 ** 23
        kids = lambda o, qs: [mm([m for gg in range(g, g + 8 // len(qs)) for m in acc(bank(5, o + 32 * gg, o + 32 + 32 * gg),
                                  [(OH[q][gg], cube("mk", 8 * q + gg, 8 * q + gg + 1, 0, 32, 32)) for q in qs])])
                              for g in range(0, 8, 8 // len(qs))]
        if t == 0:
            act(r2, bank(5, 0, 256), ACT.Identity, bias=MR); act(r3, r2, ACT.Identity, bias=-MR); tt(MB, r3, bank(5, 0, 256), ALU.not_equal)
            for u, m in ((0, N64K), (1, P64K)):
                mm([(bank(2 + u), I, MK, True, False)]
                   + [(bank(2 + u, 128 * q, 128 * q + 128), sub(HI[h], 128 * q, 128 * q + 128), m, False, q == 3) for q in range(4)])
                act(cube("mk", 0, 32, 16 * u, 16 * u + 16, 32), bank(2 + u), ACT.Relu, bias=-65536.0 if u else None)
            kids(256, range(4))
        else:
            kids(0, (2 - 2 * h, 3 - 2 * h))
            for c in range(2):
                act(sub(KB, 128 * c, 128 * c + 128), cube("p5", 0, 8, 16 * c, 16 * c + 16, 32), ACT.Sign)
            mm([(bank(3, 256 + 128 * c, 384 + 128 * c), sub(KB, 128 * c, 128 * c + 128), I, True, True) for c in range(2)])
            act(KA, bank(3, 256, 512), ACT.Copy)
            mm([m for c in range(2) for m in acc(bank(3, 128 * c, 128 * c + 128),
                                                 [(sub(C4, 0, 128), B256), (sub(KA, 128 * c, 128 * c + 128), WM)])])
            tt(bank(3, 0, 256), MB, bank(3, 0, 256), ALU.mult)
            act(r2, bank(3, 0, 256), ACT.Identity, bias=MR); act(r3, r2, ACT.Identity, bias=-MR); tt(KB, r3, bank(3, 0, 256), ALU.is_gt)
            mm([(bank(7, 256 + 128 * c, 384 + 128 * c), sub(KB, 128 * c, 128 * c + 128), N64, False, False) for c in range(2)])
            for u, m in ((0, N64K), (1, P64K)):
                mm([(bank(2, 256 * u, 256 * u + 256), I, MA, True, False)]
                   + [(bank(2, 256 * u + 128 * q, 256 * u + 128 * q + 128), sub(HI[h], 256 * h + 128 * q, 256 * h + 128 * q + 128), m, False, q == 1)
                      for q in range(2)])
            for u in range(2):
                act(cube("mk", 16 * h, 16 * h + 16, 16 * u, 16 * u + 16, 32), bank(2, 256 * u, 256 * u + 256), ACT.Relu, bias=-65536.0 if u else None)
            kids(256, (2 * h, 2 * h + 1))
        for c in range(2):
            act(sub(KS, 128 * c, 128 * c + 128), cube("p5", 8, 16, 16 * c, 16 * c + 16, 32), ACT.Copy)
            mm([(bank(7, 256 + 128 * c, 384 + 128 * c), sub(KS, 128 * c, 128 * c + 128), N64, False, False)])
        s3, b0 = bank(6, 0, 256), bank(6, 256, 512)
        add32 = [(T7, C4)] * (t < 2)
        mm(acc(b0, [(BLK, CB), (IH, e1)] + add32) + [(s3, N64, gone, True, False)])
        for c in range(4):
            n0 = 64 * c
            for u in range(2):
                mm([(bank(u), I, sub(XQ, 16 * n0 + u, 16 * n0 + 1024, 2), True, False)]
                   + [(bank(u, j, 512, 8), NI, sub(Xy, n0, n0 + 64), False, j == 7) for j in range(8)])
                act(sub(AD, 16 * n0 + u, 16 * n0 + 1024, 2), bank(u), ACT.Abs)
            tt(sub(IND, 16 * n0, 16 * n0 + 1024), ind(lm, sub(ho, n0, n0 + 64)), sub(AD, 16 * n0, 16 * n0 + 1024), ALU.is_ge)
            if c & 1:
                q = c >> 1; st = sub(ST, 128 * q, 128 * q + 128)
                mm([(bank(4, 128 * q + j, 128 * q + 128, 16), sub(IND, 2048 * q + j, 2048 * q + 2048, 16), B1, True, True) for j in range(16)])
                act(st, bank(4, 128 * q, 128 * q + 128), ACT.Copy)
                mm([(bank(7, 128 * q, 128 * q + 128), st, I, False, False), (bank(7, 256 + 128 * q, 384 + 128 * q), st, NI, False, q == 1)])
                mm([(bank(6, 128 * q, 128 * q + 128), st, NI, False, q == 1)])
        ex, c0, c31, nt2, cc = [ff(1) for _ in range(5)]
        act(ex, th1, ACT.Exp, scale=LN32, bias=math.log(22.0 / 32)); act(c0, ex, ACT.Copy, scale=-1.0)
        act(nt2, th2, ACT.Identity, scale=-1.0, bias=-64.5)
        if t:
            act(c31, ex, ACT.Copy, scale=-31.0); ts(cc, oj, c31, ALU.mult, c0, ALU.add)
        else:
            cc = c0
        act(sub(V12, 256, 512), s2, ACT.Exp, scale=LN32, bias=-128.0 * LN32)
        act(sub(V12, 0, 256), s1, ACT.Exp, scale=LN32, bias=-128.0 * LN32)
        act(drop, s3, ACT.Sign, scale=-1.0, bias=nt2)
        u1, u2 = bank(0, 0, 256), bank(3, 0, 256)
        mm([(u2, WT, sub(V12, 256, 512), True, True)])
        mm([(bank(0, 256, 512), IH, Za, True, True)]); mm([(u1, WT, sub(V12, 0, 256), True, True)])
        act(sel1, u1, ACT.Sign, scale=-1.0, bias=cc, acc=cnt if t < 2 else None); act(u2, u2, ACT.Sign, scale=-1.0, bias=-2.0 ** -90)
        tt(sw, Wm, u2, ALU.mult); tt(sq, sel1, bank(0, 256, 512), ALU.mult)
        A2, X = bank(1, 0, 256), bank(2, 0, 256)
        mm(acc(A2, [(I, gone), (NK4, C4), (W2, Wm)], True, False)); mm(acc(A2, [(NKJ, sel1), (W2, sw)], False, True))
        mm(acc(X, [(BLK, CX), (N64, FE), (BLKQ, Za), (IH, gq), (N8K, gone)] + add32, True, False))
        mm(acc(X, [(P2K, drop), (BLKN, sel1)], False, False)); mm(acc(X, [(BLKQ, sq)], False, True))
        ts(lvv, A2, 1.0, ALU.is_equal, 3071.0 if t == 2 else 3103.0, ALU.mult)
        tt(n1, lvv, b0, ALU.max)
        if t == 2:
            tt(sub(yco, 0, 512, 2), n1, X, ALU.min)
            dma("y", hbm("yc", 0, 512), yco, "s_yc", 2500)
        else:
            tt(Ch[h], n1, X, ALU.min)
            if t == 0:
                ts(e1, Ch[h], -1568.0, ALU.add); cp(sub(H2[h], 256, 512), e1)
            else:
                act(sub(yco, 1, 512, 2), Ch[1], ACT.Identity, bias=-32.0)
            act(KA, u2, ACT.Copy)
            mm(acc(bank(3, 256, 512), [(P3, inC), (P4, gone), (N4, drop), (MJ, sel1), (NI, KA)]))
            act(KB, bank(3, 256, 512), ACT.Relu, bias=3.5)
            for u, m in ((0, N64K), (1, P64K)):
                mm([x for q in range(2) for x in acc(bank(3, 256 * u + 128 * q, 256 * u + 128 * q + 128),
                    [(sub(HI[1 - h], 256 * h + 128 * q, 256 * h + 128 * q + 128), m), (sub(KB, 128 * q, 128 * q + 128), I)])])
            for u in range(2):
                act(cube("mk", 16 * h, 16 * h + 16, 16 * u, 16 * u + 16, 32), bank(3, 256 * u, 256 * u + 256), ACT.Relu, bias=-65536.0 if u else None)
            mm([(bank(5, 0, 1), ONES, cnt, True, True)])
            cp(oi, bank(5, 0, 1)); ts(oj, oi, 1, ALU.arith_shift_right, 1, ALU.bitwise_and)


def meet(a, b):
    if a[0] == b[0] and isinstance(a[5], tuple) and isinstance(b[5], tuple) and (a[5][3] <= b[5][2] or b[5][3] <= a[5][2]):
        return False
    if a[5] == b[5] == 2 and (a[3] - b[3]) % 2:
        return False
    return a[0] == b[0] and a[1] < b[2] and b[1] < a[2] and a[3] < b[4] and b[3] < a[4]


def schedule():
    n = len(OPS); dep = [set() for _ in range(n)]
    for i, o in enumerate(OPS):
        bi = set(a[0] for a in o["r"] + o["w"] if psum(a))
        o["b"] = bi
        for j in range(i):
            p = OPS[j]
            hit = any(meet(a, b) for a in o["r"] + o["w"] for b in p["w"]) or any(meet(a, b) for a in o["w"] for b in p["r"])
            if not hit and bi & p["b"] and (o["eng"] != p["eng"] or o["eng"] == "t"):
                hit = True
            if not hit and o["eng"] == p["eng"] and o["eng"] in "gy":
                hit = None
            if hit or hit is None:
                dep[i].add((j, bool(hit)))
    succ = [[] for _ in range(n)]
    for i in range(n):
        for j, w in dep[i]:
            succ[j].append((i, w))
    eng = [o["eng"] for o in OPS]; cost = [o["cost"] for o in OPS]
    hold = [0 if o["eng"] == "x" else 60 if o["sem"] else o["cost"] for o in OPS]
    lag = lambda j, i, w: (cost[j] + (0 if eng[i] == eng[j] == "t" else LAT)) if w else hold[j]
    pre = [[(j, lag(j, i, w)) for j, w in dep[i]] for i in range(n)]
    post = [[(k, lag(i, k, w)) for k, w in succ[i]] for i in range(n)]

    def place(line, t, d):
        k = 0
        while k < len(line) and line[k][1] <= t:
            k += 1
        while k < len(line) and line[k][0] < t + d:
            t = line[k][1]; k += 1
        line.insert(k, (t, t + d))
        return t

    def forward(key):
        st = [0.0] * n; lines = {}
        for i in sorted(range(n), key=lambda i: (key[i], i)):
            t = max([0.0] + [st[j] + d for j, d in pre[i]])
            st[i] = place(lines.setdefault(eng[i], []), t, hold[i]) if hold[i] else t
        return st

    def backward(st):
        en = [0.0] * n; lines = {}
        for i in sorted(range(n), key=lambda i: (-st[i], -i)):
            t = max([cost[i]] + [en[k] + d for k, d in post[i]]) - hold[i]
            en[i] = (place(lines.setdefault(eng[i], []), t, hold[i]) if hold[i] else t) + hold[i]
        return [-x for x in en]

    prio = [0.0] * n
    for i in range(n - 1, -1, -1):
        prio[i] = max([cost[i]] + [prio[k] + d for k, d in post[i]])
    rng = np.random.default_rng(1); best = cur = None; key = [-x for x in prio]
    for it in range(ROUNDS):
        st = forward(backward(forward(key))); span = max(st[i] + cost[i] for i in range(n))
        if best is None or span < best[0]:
            best = (span, st)
        if cur is None or span < cur[0] + 600 * (1 - it / ROUNDS):
            cur = (span, st)
        lo = rng.random() * cur[0]; wid = 3000 + 12000 * rng.random(); jig = rng.random(n) * 2500 * rng.random() * (rng.random(n) < 0.4)
        key = list(cur[1])
        for i in range(n):
            key[i] = max([key[i] + (float(jig[i]) if lo < key[i] < lo + wid else 0.0)] + [key[j] + 1e-3 for j, d in pre[i]])
    start = best[1]; done = [start[i] + cost[i] for i in range(n)]
    order = sorted(range(n), key=lambda i: (start[i], i))
    num = {}; know = {}; snap = [None] * n; tok = [None] * n; prog = []
    for i in order:
        o = OPS[i]; e = o["eng"]; kn = know.setdefault(e, {}); waits = []
        need = {}
        for j, w in dep[i]:
            if w and not (e == "t" == OPS[j]["eng"]) and tok[j][1] > need.get(tok[j][0], (0, 0))[0]:
                need[tok[j][0]] = (tok[j][1], j)
        for sname, (v, j) in sorted(need.items(), key=lambda z: -done[z[1][1]]):
            if kn.get(sname, 0) < v:
                waits.append((sname, v))
                for s2, v2 in snap[j].items():
                    kn[s2] = max(kn.get(s2, 0), v2)
        if o["sem"]:
            tok[i] = (o["sem"], o["val"])
        else:
            num[e] = num.get(e, 0) + 1
            tok[i] = ("n_" + e, num[e])
        snap[i] = dict(kn) if e != "x" else {}; snap[i][tok[i][0]] = tok[i][1]
        if e != "x":
            prog.append((e, waits, o["ins"], tok[i]))
    return prog, num, max(done), [(start[i], OPS[i]) for i in order]


build()
PROG, NUM, SPAN, TIMES = schedule()
SCRATCH = {k: ("sbuf", [128, v[1]], v[0]) for k, v in POOL.items()}
for _t in range(3):
    SCRATCH["d%d" % _t] = ("sbuf", [128, DW], "bfloat16")
SCRATCH.update({"mk": ("sbuf", [128, 32, 32], "bfloat16"),
                "cqi": ("sbuf", [128, 512], "int32"), "pti": ("sbuf", [128, 32], "int32"), "thi": ("sbuf", [128, 2], "int32"),
                "yco": ("sbuf", [128, 512], "float32"), "ypo": ("sbuf", [128, 32], "float32")})
for _b in range(8):
    SCRATCH["p%d" % _b] = ("psum", {4: [128, 2, 256], 5: [128, 16, 32]}.get(_b, [128, 512]), "float32")
SEMAPHORES = ["n_v", "n_s", "n_t", "n_g", "l_pt", "l_cq", "l_xs", "l_th", "l_la", "l_lb", "a_x1", "a_l1", "a_x2", "a_l2", "s_yp", "s_yc",
              "sent", "h_x", "h_l"]


def real(T, a):
    if not isap(a):
        return a
    if a[0] == "ind":
        return real(T, a[1]).indirect(real(T, a[2]))
    t = T[a[0].lstrip("@")]
    if isinstance(a[5], tuple):
        return t[:, a[5][0]:a[5][1], slice(*a[5][2:])]
    if a[0] == "p4":
        return t[:, a[3] // 256, slice(a[3] % 256, (a[4] - 1) % 256 + 1, a[5] if a[5] != 1 else None)]
    if a[0] == "p5":
        if a[4] - a[3] == 1:
            return t[:, a[3] // 32, a[3] % 32:a[4] % 32]
        return t[:, a[3] // 32:a[4] // 32, a[3] % 32:32:a[5]] if a[5] != 1 else t[:, a[3] // 32:a[4] // 32, :]
    return t[a[1]:a[2], a[3]:a[4]:a[5]] if a[5] != 1 else t[a[1]:a[2], a[3]:a[4]]


def helpers(T, topo, z):
    src = T.cores[z]
    return [c for c in topo.cores_of(src) if T.rank_of(c) is None
            and all(topo.may_write(c, T.cores[(z - t) % N]) for t in (1, 2))][:4]


def call(q, name, args, kw):
    if name == "matmul":
        return q.matmul(*args)
    if name == "tensor_scalar":
        return q.tensor_scalar(*args)
    if name == "tensor_tensor":
        return q.tensor_tensor(*args)
    if name == "tensor_copy":
        return q.tensor_copy(*args)
    if name == "memset":
        return q.memset(*args)
    if name == "activation":
        return q.activation(*args, **kw)
    if name == "iota":
        return q.iota(*args, **kw)
    return q.dma_start(*args)


def rank_program(g, core, T, topo):
    rank = T.rank_of(core)
    parts = ((TO, XP, "x"), (LO, LP, "l"))
    if rank is None:
        for z in range(N):
            hs = helpers(T, topo, z)
            if core not in hs:
                continue
            i = hs.index(core); share = len(topo.engines(T.cores[z], core)) // len(hs); sent = 0
            for t in (1, 2):
                dst = T.cores[(z - t) % N]; rid, pid = topo.addr(dst, core)
                for o, w, nm in parts:
                    if t == 1:
                        g.wait_ge(T.sem["h_" + nm], share)
                    piece = slice(o + i * w, o + (i + 1) * w)
                    g.remote_dma(T["d%d" % t][:, piece], T.d0[:, piece], T.sem["a_%s%d" % (nm, t)], T.sem.sent, pid, rid, topo.mask(core, dst))
                    sent += len(topo.engines(core, dst))
            g.wait_ge(T.sem.sent, sent)
        return
    q = {"v": g.vector, "s": g.scalar, "t": g.tensor, "g": g, "y": g.sync}
    hs = helpers(T, topo, rank); sent = 0
    for e, waits, ins, tok in PROG:
        for s, v in waits:
            q[e].wait_ge(T.sem[s], v)
        last = None
        for name, args, kw in ins:
            if name.startswith("send"):
                o, w, nm = parts[0 if name == "sendx" else 1]; tr = []
                for i, c in enumerate(hs):
                    en = topo.engines(core, c); k = len(en) // len(hs); rid, pid = topo.addr(c, core)
                    piece = slice(o + i * w, o + (i + 1) * w)
                    tr.append(RemoteDMATransfer(dst_ids=[DstId(rid=rid, pnc=pid)], dma_engine_mask=sum(1 << x for x in en[i * k:(i + 1) * k]),
                                                remote_sem=T.sem["h_" + nm], src=T.d0[:, piece], dst=T.d0[:, piece]))
                    sent += k
                g.remote_dma_fused(tr, local_sem=T.sem.sent)
            else:
                last = call(q[e], name, [real(T, a) for a in args], {k: real(T, a) for k, a in kw.items()})
        if last is not None:
            last.then_inc(T.sem[tok[0]], 16 if name == "dma_start" else 1)
    g.wait_ge(T.sem.sent, sent)
    for e in "vstg":
        g.sync.wait_ge(T.sem["n_" + e], NUM[e])
    for s in ("s_yp", "s_yc"):
        g.sync.wait_ge(T.sem[s], 16)
